import numpy as np
import ml_dtypes


def mxq(x, axis, fmt="e4m3"):
    dtype, down = {"e4m3": (ml_dtypes.float8_e4m3fn, 7), "e5m2": (ml_dtypes.float8_e5m2, 14)}[fmt]
    v = np.moveaxis(np.asarray(x, np.float32).astype(ml_dtypes.bfloat16).astype(np.float64), axis, -1)
    blocks = v.reshape(v.shape[:-1] + (-1, 32))
    amax = np.abs(blocks).max(-1, keepdims=True)
    byte = np.maximum(np.where(amax > 0, np.frexp(amax)[1] - 1 + 127, 0) - down, 1)
    scale = np.exp2(byte - 127.0)
    codes = (blocks / scale).astype(np.float32).astype(dtype).astype(np.float64)
    return np.moveaxis((codes * scale).reshape(v.shape), -1, axis)


WIDE = False


def mx_kscale(k):
    if not WIDE:
        return np.ones(k)
    levels = np.array([10, -10, 5, -5, 0])
    if k % 512:
        return np.exp2(np.random.permutation(np.resize(levels, k // 32))).repeat(32)
    a = np.empty((k // 512, 16))
    for p in range(k // 512):
        a[p, :8] = np.random.permutation(np.resize(levels, 8))
        for g in range(8):
            far = levels[np.abs(levels - a[p, g]) >= 10]
            a[p, g + 8] = far[np.random.randint(len(far))]
    return np.exp2(a.ravel()).repeat(32)


def f64(x):
    return np.asarray(x).astype(np.float64)


def striped(idx):
    return np.tile(idx.reshape(-1, 16).T, (8, 1)).astype(np.uint16)


def unstriped(offs):
    return offs[:16].T.reshape(-1).astype(np.int64)


K, T, S, V, N = 512, 4096, 1024, 512, 256


def setup_inputs():
    n = np.random.standard_normal
    s = mx_kscale(K)[:, None]
    return {
        "xT": (n((K, T)) * s).astype(np.float32),
        "sT": (n((K, V)) * s).astype(np.float32),
        "w1": (n((K, N)) / np.sqrt(K) / s).astype(np.float32),
        "w2": (n((K, N)) / np.sqrt(K) / s).astype(np.float32),
        "offs": striped(np.random.permutation(T)[:S]),
        "par": striped(np.random.randint(0, V, S)),
    }


def reference(xT, sT, w1, w2, offs, par):
    xq = mxq(f64(xT)[:, unstriped(offs)], 0, "e4m3")
    y = mxq(f64(w1), 0, "e4m3").T @ xq
    t = mxq(f64(w2), 0, "e4m3").T @ mxq(f64(sT), 0, "e4m3")
    return y + t[:, unstriped(par)]

@@ -1,0 +1,165 @@
+from contextlib import ExitStack
+
+import concourse.mybir as mybir
+
+K, T, S, V, N = 512, 4096, 1024, 512, 256
+FLOPS = 2 * K * N * (S + V)
+
+F32 = mybir.dt.float32
+BF16 = mybir.dt.bfloat16
+U32 = mybir.dt.uint32
+U16 = mybir.dt.uint16
+U8 = mybir.dt.uint8
+FP8X4 = mybir.dt.float8_e4m3fn_x4
+COPY = mybir.ActivationFunctionType.Copy
+ADD = mybir.AluOpType.add
+
+P = 128
+PACK = 4
+LIST_ROWS = 16
+HALF = S // 2
+PIECE = 256
+M_TILES = N // P
+PAIR_CHUNK = 1024
+LAST_CHUNKS = (1024, 1024, 1024, 512, 512)
+VECTOR_CHUNK = 3
+
+
+def entries(list_tile, first, count):
+    return list_tile[:, first // LIST_ROWS : (first + count) // LIST_ROWS]
+
+
+def interleave(nc, grouped, raw):
+    nc.vector.tensor_copy(
+        out=grouped[:].rearrange("p (c i t) -> p c t i", i=4, t=PACK),
+        in_=raw[:].rearrange("p t (c i) -> p c t i", i=4),
+    )
+
+
+def tile_picked_fpn_none_e_kernel(tc, xT, sT, w1, w2, offs, par, out):
+    nc = tc.nc
+    x_rows = xT.rearrange("(p t) c -> p t c", t=PACK)
+    out_rows = out.rearrange("(m p) j -> p m j", p=P)
+
+    with ExitStack() as ctx:
+        sb = ctx.enter_context(tc.tile_pool(name="sb", bufs=1))
+        ps = ctx.enter_context(tc.psum_pool(name="ps", bufs=1))
+
+        def load_packed(name, src, width):
+            raw = sb.tile([P, PACK, width], F32, name=name + "_raw")
+            nc.sync.dma_start(out=raw[:], in_=src.rearrange("(p t) c -> p t c", t=PACK))
+            return raw
+
+        ring = ctx.enter_context(tc.tile_pool(name="ring", bufs=2))
+
+        def quantize(name, grouped, width, pool=sb):
+            codes = pool.tile([P, width], U32, name=name + "_codes", align_bytes=64)
+            scales = pool.tile([P, width], U8, name=name + "_scales", align_bytes=64)
+            nc.vector.quantize_mx(out=codes[:].bitcast(FP8X4), scales=scales[:], in_=grouped)
+            return codes, scales
+
+        def quantize_plain(name, raw, width):
+            grouped = sb.tile([P, width * PACK], BF16, name=name + "_grouped", align_bytes=64)
+            interleave(nc, grouped, raw)
+            return quantize(name, grouped[:], width)
+
+        def product(acc, w, m, x):
+            cols = slice(m * P, (m + 1) * P)
+            nc.tensor.matmul_mx(
+                out=acc,
+                lhsT=w[0][:, cols].bitcast(FP8X4),
+                lhsT_scale=w[1][:, cols],
+                rhs=x[0][:].bitcast(FP8X4),
+                rhs_scale=x[1][:],
+                start=True,
+                stop=True,
+            )
+
+        w2_raw = load_packed("w2", w2, N)
+        s_raw = load_packed("s", sT, V)
+        par_tile = sb.tile([P, S // LIST_ROWS], U16, name="par_tile")
+        nc.sync.dma_start(par_tile[:], par)
+        offs_tile = sb.tile([P, S // LIST_ROWS], U16, name="offs_tile")
+        nc.sync.dma_start(offs_tile[:], offs)
+        low_raw = []
+        for c0 in range(0, T, PAIR_CHUNK):
+            raw = sb.tile([P, 2, PAIR_CHUNK], F32, name="low_raw%d" % c0)
+            nc.sync.dma_start(out=raw[:], in_=x_rows[:, 0:2, c0 : c0 + PAIR_CHUNK])
+            low_raw.append(raw)
+        w1_raw = load_packed("w1", w1, N)
+        row2 = sb.tile([P, T], F32, name="row2")
+        nc.sync.dma_start(out=row2[:], in_=x_rows[:, 2, :])
+        row3 = sb.tile([P, T], F32, name="row3")
+        c0 = 0
+        last_cols = []
+        for width in LAST_CHUNKS:
+            cols = slice(c0, c0 + width)
+            nc.sync.dma_start(out=row3[:, cols], in_=x_rows[:, 3, cols])
+            last_cols.append(cols)
+            c0 = c0 + width
+
+        w2_mx = quantize_plain("w2", w2_raw, N)
+        s_mx = quantize_plain("s", s_raw, V)
+        parents = sb.tile([P, S // PIECE, M_TILES, PIECE], F32, name="parents")
+        coarse = []
+        for m in range(M_TILES):
+            acc = ps.tile([P, V], F32, name="coarse_acc%d" % m)
+            product(acc[:], w2_mx, m, s_mx)
+            t_rows = sb.tile([P, V], F32, name="coarse%d" % m)
+            nc.vector.tensor_copy(out=t_rows[:], in_=acc[:])
+            coarse.append(t_rows)
+        for m in range(M_TILES):
+            for piece in range(S // PIECE):
+                nc.vector.tensor_copy(
+                    parents[:, piece, m, :], coarse[m][:].indirect(entries(par_tile, piece * PIECE, PIECE))
+                )
+
+        pairs = sb.tile([P, 2 * T], BF16, name="pairs")
+        for index, raw in enumerate(low_raw):
+            c0 = index * PAIR_CHUNK
+            nc.scalar.copy(
+                out=pairs[:, 2 * c0 : 2 * (c0 + PAIR_CHUNK)].rearrange("p (c t) -> p c t", t=2),
+                in_=raw[:].rearrange("p t c -> p c t"),
+            )
+        w1_mx = quantize_plain("w1", w1_raw, N)
+
+        picked = [sb.tile([P, HALF * PACK], BF16, name="picked%d" % h, align_bytes=64) for h in range(2)]
+
+        def slot(h, t):
+            return picked[h][:].rearrange("p (c t) -> p c t", t=PACK)[:, :, t]
+
+        for h in range(2):
+            words = picked[h][:].bitcast(U32).rearrange("p (c u) -> p c u", u=2)[:, :, 0]
+            nc.vector.tensor_copy(words, pairs[:].bitcast(U32).indirect(entries(offs_tile, h * HALF, HALF)))
+        for h in (1, 0):
+            nc.vector.tensor_copy(slot(h, 2), row2[:].indirect(entries(offs_tile, h * HALF, HALF)))
+
+        row3_bf = sb.tile([P, T], BF16, name="row3_bf")
+        for index, cols in enumerate(last_cols):
+            if index == VECTOR_CHUNK:
+                nc.vector.tensor_copy(out=row3_bf[:, cols], in_=row3[:, cols])
+            else:
+                nc.scalar.copy(out=row3_bf[:, cols], in_=row3[:, cols])
+
+        nc.vector.tensor_copy(slot(0, 3), row3[:].indirect(entries(offs_tile, 0, HALF)))
+        nc.scalar.activation(slot(1, 3), row3_bf[:].indirect(entries(offs_tile, HALF, HALF)), COPY)
+
+        def fine_product(piece):
+            h, inner = divmod(piece, HALF // PIECE)
+            grouped = picked[h][:, inner * PIECE * PACK : (inner + 1) * PIECE * PACK]
+            x_mx = quantize("x", grouped, PIECE, ring)
+            acc = ps.tile([P, M_TILES, PIECE], F32, name="fine_acc%d" % piece)
+            for m in range(M_TILES):
+                product(acc[:, m, :], w1_mx, m, x_mx)
+            return acc
+
+        def finish(piece, acc):
+            result = sb.tile([P, M_TILES, PIECE], F32, name="result%d" % piece)
+            nc.vector.tensor_tensor(result[:], acc[:], parents[:, piece, :, :], ADD)
+            nc.sync.dma_start(out=out_rows[:, :, piece * PIECE : (piece + 1) * PIECE], in_=result[:])
+
+        accs = [fine_product(0), fine_product(1)]
+        for piece in range(S // PIECE):
+            finish(piece, accs[piece])
+            if piece + 2 < S // PIECE:
+                accs.append(fine_product(piece + 2))

@@ -20,26 +20,25 @@ LIST_ROWS = 16
 HALF = S // 2
 PIECE = 256
 M_TILES = N // P
-PAIR_CHUNK = 1024
-LAST_CHUNKS = (1024, 1024, 1024, 512, 512)
-VECTOR_CHUNK = 3
+LAST_CHUNKS = (1024, 1024, 1024, 512, 256, 256)
+VECTOR_CHUNKS = (3, 4)
+S_SPLIT = 320
 
 
 def entries(list_tile, first, count):
     return list_tile[:, first // LIST_ROWS : (first + count) // LIST_ROWS]
 
 
-def interleave(nc, grouped, raw):
-    nc.vector.tensor_copy(
-        out=grouped[:].rearrange("p (c i t) -> p c t i", i=4, t=PACK),
-        in_=raw[:].rearrange("p t (c i) -> p c t i", i=4),
+def interleave(copy, grouped, raw, first, last):
+    copy(
+        out=grouped[:, first * PACK : last * PACK].rearrange("p (c i t) -> p c t i", i=4, t=PACK),
+        in_=raw[:, :, first:last].rearrange("p t (c i) -> p c t i", i=4),
     )
 
 
 def tile_picked_fpn_none_e_kernel(tc, xT, sT, w1, w2, offs, par, out):
     nc = tc.nc
     x_rows = xT.rearrange("(p t) c -> p t c", t=PACK)
-    out_rows = out.rearrange("(m p) j -> p m j", p=P)
 
     with ExitStack() as ctx:
         sb = ctx.enter_context(tc.tile_pool(name="sb", bufs=1))
@@ -50,17 +49,18 @@ def tile_picked_fpn_none_e_kernel(tc, xT, sT, w1, w2, offs, par, out):
             nc.sync.dma_start(out=raw[:], in_=src.rearrange("(p t) c -> p t c", t=PACK))
             return raw
 
-        ring = ctx.enter_context(tc.tile_pool(name="ring", bufs=2))
-
-        def quantize(name, grouped, width, pool=sb):
-            codes = pool.tile([P, width], U32, name=name + "_codes", align_bytes=64)
-            scales = pool.tile([P, width], U8, name=name + "_scales", align_bytes=64)
+        def quantize(name, grouped, width):
+            codes = sb.tile([P, width], U32, name=name + "_codes", align_bytes=64)
+            scales = sb.tile([P, width], U8, name=name + "_scales", align_bytes=64)
             nc.vector.quantize_mx(out=codes[:].bitcast(FP8X4), scales=scales[:], in_=grouped)
             return codes, scales
 
-        def quantize_plain(name, raw, width):
+        def quantize_plain(name, raw, width, split):
             grouped = sb.tile([P, width * PACK], BF16, name=name + "_grouped", align_bytes=64)
-            interleave(nc, grouped, raw)
+            if split > 0:
+                interleave(nc.vector.tensor_copy, grouped, raw, 0, split)
+            if split < width:
+                interleave(nc.scalar.copy, grouped, raw, split, width)
             return quantize(name, grouped[:], width)
 
         def product(acc, w, m, x):
@@ -81,12 +81,11 @@ def tile_picked_fpn_none_e_kernel(tc, xT, sT, w1, w2, offs, par, out):
         nc.sync.dma_start(par_tile[:], par)
         offs_tile = sb.tile([P, S // LIST_ROWS], U16, name="offs_tile")
         nc.sync.dma_start(offs_tile[:], offs)
-        low_raw = []
-        for c0 in range(0, T, PAIR_CHUNK):
-            raw = sb.tile([P, 2, PAIR_CHUNK], F32, name="low_raw%d" % c0)
-            nc.sync.dma_start(out=raw[:], in_=x_rows[:, 0:2, c0 : c0 + PAIR_CHUNK])
-            low_raw.append(raw)
+        row0 = sb.tile([P, T], F32, name="row0")
+        nc.sync.dma_start(out=row0[:], in_=x_rows[:, 0, :])
         w1_raw = load_packed("w1", w1, N)
+        row1 = sb.tile([P, T], F32, name="row1", tag="row1")
+        nc.sync.dma_start(out=row1[:], in_=x_rows[:, 1, :])
         row2 = sb.tile([P, T], F32, name="row2")
         nc.sync.dma_start(out=row2[:], in_=x_rows[:, 2, :])
         row3 = sb.tile([P, T], F32, name="row3")
@@ -98,45 +97,48 @@ def tile_picked_fpn_none_e_kernel(tc, xT, sT, w1, w2, offs, par, out):
             last_cols.append(cols)
             c0 = c0 + width
 
-        w2_mx = quantize_plain("w2", w2_raw, N)
-        s_mx = quantize_plain("s", s_raw, V)
-        parents = sb.tile([P, S // PIECE, M_TILES, PIECE], F32, name="parents")
+        w2_mx = quantize_plain("w2", w2_raw, N, N)
+        s_mx = quantize_plain("s", s_raw, V, S_SPLIT)
         coarse = []
         for m in range(M_TILES):
             acc = ps.tile([P, V], F32, name="coarse_acc%d" % m)
             product(acc[:], w2_mx, m, s_mx)
             t_rows = sb.tile([P, V], F32, name="coarse%d" % m)
-            nc.vector.tensor_copy(out=t_rows[:], in_=acc[:])
+            nc.scalar.copy(out=t_rows[:], in_=acc[:])
             coarse.append(t_rows)
-        for m in range(M_TILES):
-            for piece in range(S // PIECE):
-                nc.vector.tensor_copy(
-                    parents[:, piece, m, :], coarse[m][:].indirect(entries(par_tile, piece * PIECE, PIECE))
-                )
 
-        pairs = sb.tile([P, 2 * T], BF16, name="pairs")
-        for index, raw in enumerate(low_raw):
-            c0 = index * PAIR_CHUNK
-            nc.scalar.copy(
-                out=pairs[:, 2 * c0 : 2 * (c0 + PAIR_CHUNK)].rearrange("p (c t) -> p c t", t=2),
-                in_=raw[:].rearrange("p t c -> p c t"),
-            )
-        w1_mx = quantize_plain("w1", w1_raw, N)
+        def fetch_parents(h, tag):
+            parents = sb.tile([P, M_TILES, HALF], F32, name="parents%d" % h, tag=tag)
+            for m in range(M_TILES):
+                for c0 in range(0, HALF, PIECE):
+                    window = coarse[m][:].indirect(entries(par_tile, h * HALF + c0, PIECE))
+                    nc.vector.tensor_copy(parents[:, m, c0 : c0 + PIECE], window)
+            return parents
+
+        parent_halves = [fetch_parents(0, "parents0")]
 
         picked = [sb.tile([P, HALF * PACK], BF16, name="picked%d" % h, align_bytes=64) for h in range(2)]
 
         def slot(h, t):
             return picked[h][:].rearrange("p (c t) -> p c t", t=PACK)[:, :, t]
 
+        low = sb.tile([P, 2, S], BF16, name="low")
+        nc.vector.tensor_copy(low[:, 0, :], row0[:].indirect(offs_tile[:]))
+        w1_mx = quantize_plain("w1", w1_raw, N, 0)
         for h in range(2):
-            words = picked[h][:].bitcast(U32).rearrange("p (c u) -> p c u", u=2)[:, :, 0]
-            nc.vector.tensor_copy(words, pairs[:].bitcast(U32).indirect(entries(offs_tile, h * HALF, HALF)))
+            cols = slice(h * HALF, (h + 1) * HALF)
+            nc.vector.tensor_copy(low[:, 1, cols], row1[:].indirect(entries(offs_tile, h * HALF, HALF)))
+            nc.scalar.copy(
+                out=picked[h][:].rearrange("p (c t) -> p c t", t=PACK)[:, :, 0:2],
+                in_=low[:, :, cols].rearrange("p t c -> p c t"),
+            )
+        parent_halves.append(fetch_parents(1, "row1"))
         for h in (1, 0):
             nc.vector.tensor_copy(slot(h, 2), row2[:].indirect(entries(offs_tile, h * HALF, HALF)))
 
         row3_bf = sb.tile([P, T], BF16, name="row3_bf")
         for index, cols in enumerate(last_cols):
-            if index == VECTOR_CHUNK:
+            if index in VECTOR_CHUNKS:
                 nc.vector.tensor_copy(out=row3_bf[:, cols], in_=row3[:, cols])
             else:
                 nc.scalar.copy(out=row3_bf[:, cols], in_=row3[:, cols])
@@ -144,22 +146,14 @@ def tile_picked_fpn_none_e_kernel(tc, xT, sT, w1, w2, offs, par, out):
         nc.vector.tensor_copy(slot(0, 3), row3[:].indirect(entries(offs_tile, 0, HALF)))
         nc.scalar.activation(slot(1, 3), row3_bf[:].indirect(entries(offs_tile, HALF, HALF)), COPY)
 
-        def fine_product(piece):
-            h, inner = divmod(piece, HALF // PIECE)
-            grouped = picked[h][:, inner * PIECE * PACK : (inner + 1) * PIECE * PACK]
-            x_mx = quantize("x", grouped, PIECE, ring)
-            acc = ps.tile([P, M_TILES, PIECE], F32, name="fine_acc%d" % piece)
+        accs = [[ps.tile([P, HALF], F32, name="fine_acc%d_%d" % (h, m)) for m in range(M_TILES)] for h in range(2)]
+        for h in range(2):
+            for c0 in range(0, HALF, PIECE):
+                x_mx = quantize("x%d_%d" % (h, c0), picked[h][:, c0 * PACK : (c0 + PIECE) * PACK], PIECE)
+                for m in range(M_TILES):
+                    product(accs[h][m][:, c0 : c0 + PIECE], w1_mx, m, x_mx)
+        for h in range(2):
             for m in range(M_TILES):
-                product(acc[:, m, :], w1_mx, m, x_mx)
-            return acc
-
-        def finish(piece, acc):
-            result = sb.tile([P, M_TILES, PIECE], F32, name="result%d" % piece)
-            nc.vector.tensor_tensor(result[:], acc[:], parents[:, piece, :, :], ADD)
-            nc.sync.dma_start(out=out_rows[:, :, piece * PIECE : (piece + 1) * PIECE], in_=result[:])
-
-        accs = [fine_product(0), fine_product(1)]
-        for piece in range(S // PIECE):
-            finish(piece, accs[piece])
-            if piece + 2 < S // PIECE:
-                accs.append(fine_product(piece + 2))
+                result = sb.tile([P, HALF], F32, name="result%d_%d" % (h, m))
+                nc.vector.tensor_tensor(result[:], accs[h][m][:], parent_halves[h][:, m, :], ADD)
+                nc.sync.dma_start(out=out[m * P : (m + 1) * P, h * HALF : (h + 1) * HALF], in_=result[:])

@@ -45,7 +45,7 @@ def tile_picked_fpn_none_e_kernel(tc, xT, sT, w1, w2, offs, par, out):
         ps = ctx.enter_context(tc.psum_pool(name="ps", bufs=1))
 
         def load_packed(name, src, width):
-            raw = sb.tile([P, PACK, width], F32, name=name + "_raw")
+            raw = sb.tile([P, PACK, width], F32, name=name + "_raw", tag=name + "_raw", align_bytes=64)
             nc.sync.dma_start(out=raw[:], in_=src.rearrange("(p t) c -> p t c", t=PACK))
             return raw
 
@@ -69,8 +69,8 @@ def tile_picked_fpn_none_e_kernel(tc, xT, sT, w1, w2, offs, par, out):
                 out=acc,
                 lhsT=w[0][:, cols].bitcast(FP8X4),
                 lhsT_scale=w[1][:, cols],
-                rhs=x[0][:].bitcast(FP8X4),
-                rhs_scale=x[1][:],
+                rhs=x[0].bitcast(FP8X4),
+                rhs_scale=x[1],
                 start=True,
                 stop=True,
             )
@@ -83,7 +83,6 @@ def tile_picked_fpn_none_e_kernel(tc, xT, sT, w1, w2, offs, par, out):
         nc.sync.dma_start(offs_tile[:], offs)
         row0 = sb.tile([P, T], F32, name="row0")
         nc.sync.dma_start(out=row0[:], in_=x_rows[:, 0, :])
-        w1_raw = load_packed("w1", w1, N)
         row1 = sb.tile([P, T], F32, name="row1", tag="row1")
         nc.sync.dma_start(out=row1[:], in_=x_rows[:, 1, :])
         row2 = sb.tile([P, T], F32, name="row2")
@@ -96,13 +95,14 @@ def tile_picked_fpn_none_e_kernel(tc, xT, sT, w1, w2, offs, par, out):
             nc.sync.dma_start(out=row3[:, cols], in_=x_rows[:, 3, cols])
             last_cols.append(cols)
             c0 = c0 + width
+        w1_raw = [load_packed("w1_%d" % m, w1[:, m * P : (m + 1) * P], P) for m in range(M_TILES)]
 
         w2_mx = quantize_plain("w2", w2_raw, N, N)
         s_mx = quantize_plain("s", s_raw, V, S_SPLIT)
         coarse = []
         for m in range(M_TILES):
             acc = ps.tile([P, V], F32, name="coarse_acc%d" % m)
-            product(acc[:], w2_mx, m, s_mx)
+            product(acc[:], w2_mx, m, (s_mx[0][:], s_mx[1][:]))
             t_rows = sb.tile([P, V], F32, name="coarse%d" % m)
             nc.scalar.copy(out=t_rows[:], in_=acc[:])
             coarse.append(t_rows)
@@ -124,7 +124,6 @@ def tile_picked_fpn_none_e_kernel(tc, xT, sT, w1, w2, offs, par, out):
 
         low = sb.tile([P, 2, S], BF16, name="low")
         nc.vector.tensor_copy(low[:, 0, :], row0[:].indirect(offs_tile[:]))
-        w1_mx = quantize_plain("w1", w1_raw, N, 0)
         for h in range(2):
             cols = slice(h * HALF, (h + 1) * HALF)
             nc.vector.tensor_copy(low[:, 1, cols], row1[:].indirect(entries(offs_tile, h * HALF, HALF)))
@@ -147,13 +146,40 @@ def tile_picked_fpn_none_e_kernel(tc, xT, sT, w1, w2, offs, par, out):
         nc.scalar.activation(slot(1, 3), row3_bf[:].indirect(entries(offs_tile, HALF, HALF)), COPY)
 
         accs = [[ps.tile([P, HALF], F32, name="fine_acc%d_%d" % (h, m)) for m in range(M_TILES)] for h in range(2)]
-        for h in range(2):
-            for c0 in range(0, HALF, PIECE):
-                x_mx = quantize("x%d_%d" % (h, c0), picked[h][:, c0 * PACK : (c0 + PIECE) * PACK], PIECE)
-                for m in range(M_TILES):
-                    product(accs[h][m][:, c0 : c0 + PIECE], w1_mx, m, x_mx)
-        for h in range(2):
-            for m in range(M_TILES):
-                result = sb.tile([P, HALF], F32, name="result%d_%d" % (h, m))
-                nc.vector.tensor_tensor(result[:], accs[h][m][:], parent_halves[h][:, m, :], ADD)
-                nc.sync.dma_start(out=out[m * P : (m + 1) * P, h * HALF : (h + 1) * HALF], in_=result[:])
+        w1_grouped = [sb.tile([P, P * PACK], BF16, name="w1_grouped%d" % m, align_bytes=64) for m in range(M_TILES)]
+        interleave(nc.vector.tensor_copy, w1_grouped[0], w1_raw[0], 0, P)
+        interleave(nc.scalar.copy, w1_grouped[1], w1_raw[1], 0, P)
+        x_codes = sb.tile([P, S], U32, name="x_codes", tag="w1_0_raw", align_bytes=64)
+        x_scales = sb.tile([P, S], U8, name="x_scales", align_bytes=64)
+
+        def quantize_piece(first):
+            h, c0 = divmod(first, HALF)
+            cols = slice(first, first + PIECE)
+            nc.vector.quantize_mx(
+                out=x_codes[:, cols].bitcast(FP8X4),
+                scales=x_scales[:, cols],
+                in_=picked[h][:, c0 * PACK : (c0 + PIECE) * PACK],
+            )
+
+        def fine_products(w_mx, m, first):
+            h, c0 = divmod(first, HALF)
+            x_mx = (x_codes[:, first : first + PIECE], x_scales[:, first : first + PIECE])
+            product(accs[h][m][:, c0 : c0 + PIECE], w_mx, 0, x_mx)
+
+        def finish(h, m):
+            result = sb.tile([P, HALF], F32, name="result%d_%d" % (h, m))
+            nc.vector.tensor_tensor(result[:], accs[h][m][:], parent_halves[h][:, m, :], ADD)
+            nc.sync.dma_start(out=out[m * P : (m + 1) * P, h * HALF : (h + 1) * HALF], in_=result[:])
+
+        quantize_piece(0)
+        w1_mx = quantize("w1_0", w1_grouped[0][:], P)
+        for first in range(0, S, PIECE):
+            if first > 0:
+                quantize_piece(first)
+            fine_products(w1_mx, 0, first)
+        w1_mx = quantize("w1_1", w1_grouped[1][:], P)
+        for first in range(0, S, PIECE):
+            fine_products(w1_mx, 1, first)
+        for m in range(M_TILES):
+            for h in range(2):
+                finish(h, m)

@@ -20,8 +20,8 @@ LIST_ROWS = 16
 HALF = S // 2
 PIECE = 256
 M_TILES = N // P
-LAST_CHUNKS = (1024, 1024, 1024, 512, 256, 256)
-VECTOR_CHUNKS = (3, 4)
+LAST_CHUNKS = (1024, 1024, 1024, 512, 512)
+VECTOR_CHUNKS = (3,)
 S_SPLIT = 320
 
 
@@ -75,8 +75,8 @@ def tile_picked_fpn_none_e_kernel(tc, xT, sT, w1, w2, offs, par, out):
                 stop=True,
             )
 
-        w2_raw = load_packed("w2", w2, N)
         s_raw = load_packed("s", sT, V)
+        w2_raw = load_packed("w2", w2, N)
         par_tile = sb.tile([P, S // LIST_ROWS], U16, name="par_tile")
         nc.sync.dma_start(par_tile[:], par)
         offs_tile = sb.tile([P, S // LIST_ROWS], U16, name="offs_tile")
@@ -97,8 +97,8 @@ def tile_picked_fpn_none_e_kernel(tc, xT, sT, w1, w2, offs, par, out):
             c0 = c0 + width
         w1_raw = [load_packed("w1_%d" % m, w1[:, m * P : (m + 1) * P], P) for m in range(M_TILES)]
 
-        w2_mx = quantize_plain("w2", w2_raw, N, N)
         s_mx = quantize_plain("s", s_raw, V, S_SPLIT)
+        w2_mx = quantize_plain("w2", w2_raw, N, S_SPLIT // 2)
         coarse = []
         for m in range(M_TILES):
             acc = ps.tile([P, V], F32, name="coarse_acc%d" % m)
@@ -107,15 +107,14 @@ def tile_picked_fpn_none_e_kernel(tc, xT, sT, w1, w2, offs, par, out):
             nc.scalar.copy(out=t_rows[:], in_=acc[:])
             coarse.append(t_rows)
 
-        def fetch_parents(h, tag):
-            parents = sb.tile([P, M_TILES, HALF], F32, name="parents%d" % h, tag=tag)
-            for m in range(M_TILES):
-                for c0 in range(0, HALF, PIECE):
-                    window = coarse[m][:].indirect(entries(par_tile, h * HALF + c0, PIECE))
-                    nc.vector.tensor_copy(parents[:, m, c0 : c0 + PIECE], window)
+        def fetch_parents(h, m, tag):
+            parents = sb.tile([P, HALF], F32, name="parents%d_%d" % (h, m), tag=tag)
+            for c0 in range(0, HALF, PIECE):
+                window = coarse[m][:].indirect(entries(par_tile, h * HALF + c0, PIECE))
+                nc.vector.tensor_copy(parents[:, c0 : c0 + PIECE], window)
             return parents
 
-        parent_halves = [fetch_parents(0, "parents0")]
+        parents = {(h, m): fetch_parents(h, m, "parents%d_%d" % (h, m)) for h, m in ((0, 0), (1, 0), (0, 1))}
 
         picked = [sb.tile([P, HALF * PACK], BF16, name="picked%d" % h, align_bytes=64) for h in range(2)]
 
@@ -131,7 +130,7 @@ def tile_picked_fpn_none_e_kernel(tc, xT, sT, w1, w2, offs, par, out):
                 out=picked[h][:].rearrange("p (c t) -> p c t", t=PACK)[:, :, 0:2],
                 in_=low[:, :, cols].rearrange("p t c -> p c t"),
             )
-        parent_halves.append(fetch_parents(1, "row1"))
+        parents.setdefault((1, 1), fetch_parents(1, 1, "row1"))
         for h in (1, 0):
             nc.vector.tensor_copy(slot(h, 2), row2[:].indirect(entries(offs_tile, h * HALF, HALF)))
 
@@ -168,7 +167,7 @@ def tile_picked_fpn_none_e_kernel(tc, xT, sT, w1, w2, offs, par, out):
 
         def finish(h, m):
             result = sb.tile([P, HALF], F32, name="result%d_%d" % (h, m))
-            nc.vector.tensor_tensor(result[:], accs[h][m][:], parent_halves[h][:, m, :], ADD)
+            nc.vector.tensor_tensor(result[:], accs[h][m][:], parents[h, m][:], ADD)
             nc.sync.dma_start(out=out[m * P : (m + 1) * P, h * HALF : (h + 1) * HALF], in_=result[:])
 
         quantize_piece(0)

@@ -20,8 +20,8 @@ LIST_ROWS = 16
 HALF = S // 2
 PIECE = 256
 M_TILES = N // P
-LAST_CHUNKS = (1024, 1024, 1024, 512, 512)
-VECTOR_CHUNKS = (3,)
+LAST_CHUNKS = (1024, 1024, 1024, 512, 256, 256)
+VECTOR_CHUNKS = (3, 4)
 S_SPLIT = 320
 
 
@@ -43,6 +43,9 @@ def tile_picked_fpn_none_e_kernel(tc, xT, sT, w1, w2, offs, par, out):
     with ExitStack() as ctx:
         sb = ctx.enter_context(tc.tile_pool(name="sb", bufs=1))
         ps = ctx.enter_context(tc.psum_pool(name="ps", bufs=1))
+
+        def gpsimd_copy(out, in_):
+            nc.gpsimd.tensor_scalar(out=out, in0=in_, scalar1=1.0, scalar2=0.0, op0=mybir.AluOpType.mult, op1=ADD)
 
         def load_packed(name, src, width):
             raw = sb.tile([P, PACK, width], F32, name=name + "_raw", tag=name + "_raw", align_bytes=64)
@@ -146,7 +149,7 @@ def tile_picked_fpn_none_e_kernel(tc, xT, sT, w1, w2, offs, par, out):
 
         accs = [[ps.tile([P, HALF], F32, name="fine_acc%d_%d" % (h, m)) for m in range(M_TILES)] for h in range(2)]
         w1_grouped = [sb.tile([P, P * PACK], BF16, name="w1_grouped%d" % m, align_bytes=64) for m in range(M_TILES)]
-        interleave(nc.vector.tensor_copy, w1_grouped[0], w1_raw[0], 0, P)
+        gpsimd_copy(w1_grouped[0][:].rearrange("p (c t) -> p c t", t=PACK), w1_raw[0][:].rearrange("p t c -> p c t"))
         interleave(nc.scalar.copy, w1_grouped[1], w1_raw[1], 0, P)
         x_codes = sb.tile([P, S], U32, name="x_codes", tag="w1_0_raw", align_bytes=64)
         x_scales = sb.tile([P, S], U8, name="x_scales", align_bytes=64)
@@ -170,11 +173,9 @@ def tile_picked_fpn_none_e_kernel(tc, xT, sT, w1, w2, offs, par, out):
             nc.vector.tensor_tensor(result[:], accs[h][m][:], parents[h, m][:], ADD)
             nc.sync.dma_start(out=out[m * P : (m + 1) * P, h * HALF : (h + 1) * HALF], in_=result[:])
 
-        quantize_piece(0)
         w1_mx = quantize("w1_0", w1_grouped[0][:], P)
         for first in range(0, S, PIECE):
-            if first > 0:
-                quantize_piece(first)
+            quantize_piece(first)
             fine_products(w1_mx, 0, first)
         w1_mx = quantize("w1_1", w1_grouped[1][:], P)
         for first in range(0, S, PIECE):

@@ -147,7 +147,6 @@ def tile_picked_fpn_none_e_kernel(tc, xT, sT, w1, w2, offs, par, out):
         nc.vector.tensor_copy(slot(0, 3), row3[:].indirect(entries(offs_tile, 0, HALF)))
         nc.scalar.activation(slot(1, 3), row3_bf[:].indirect(entries(offs_tile, HALF, HALF)), COPY)
 
-        accs = [[ps.tile([P, HALF], F32, name="fine_acc%d_%d" % (h, m)) for m in range(M_TILES)] for h in range(2)]
         w1_grouped = [sb.tile([P, P * PACK], BF16, name="w1_grouped%d" % m, align_bytes=64) for m in range(M_TILES)]
         gpsimd_copy(w1_grouped[0][:].rearrange("p (c t) -> p c t", t=PACK), w1_raw[0][:].rearrange("p t c -> p c t"))
         interleave(nc.scalar.copy, w1_grouped[1], w1_raw[1], 0, P)
@@ -163,23 +162,24 @@ def tile_picked_fpn_none_e_kernel(tc, xT, sT, w1, w2, offs, par, out):
                 in_=picked[h][:, c0 * PACK : (c0 + PIECE) * PACK],
             )
 
-        def fine_products(w_mx, m, first):
+        def fine_product(w_mx, m, first, count):
+            acc = ps.tile([P, count], F32, name="fine_acc%d_%d" % (m, first))
+            product(acc[:], w_mx, 0, (x_codes[:, first : first + count], x_scales[:, first : first + count]))
+            return acc
+
+        def finish(acc, m, first, count):
             h, c0 = divmod(first, HALF)
-            x_mx = (x_codes[:, first : first + PIECE], x_scales[:, first : first + PIECE])
-            product(accs[h][m][:, c0 : c0 + PIECE], w_mx, 0, x_mx)
+            result = sb.tile([P, count], F32, name="result%d_%d" % (m, first))
+            nc.vector.tensor_tensor(result[:], acc[:], parents[h, m][:, c0 : c0 + count], ADD)
+            nc.sync.dma_start(out=out[m * P : (m + 1) * P, first : first + count], in_=result[:])
 
-        def finish(h, m):
-            result = sb.tile([P, HALF], F32, name="result%d_%d" % (h, m))
-            nc.vector.tensor_tensor(result[:], accs[h][m][:], parents[h, m][:], ADD)
-            nc.sync.dma_start(out=out[m * P : (m + 1) * P, h * HALF : (h + 1) * HALF], in_=result[:])
-
+        units = []
         w1_mx = quantize("w1_0", w1_grouped[0][:], P)
         for first in range(0, S, PIECE):
             quantize_piece(first)
-            fine_products(w1_mx, 0, first)
+            units.append((fine_product(w1_mx, 0, first, PIECE), 0, first, PIECE))
         w1_mx = quantize("w1_1", w1_grouped[1][:], P)
-        for first in range(0, S, PIECE):
-            fine_products(w1_mx, 1, first)
-        for m in range(M_TILES):
-            for h in range(2):
-                finish(h, m)
+        for first in range(0, S, HALF):
+            units.append((fine_product(w1_mx, 1, first, HALF), 1, first, HALF))
+        for unit in units:
+            finish(*unit)

@@ -20,7 +20,7 @@ LIST_ROWS = 16
 HALF = S // 2
 PIECE = 256
 M_TILES = N // P
-LAST_CHUNKS = (1024, 1024, 1024, 512, 256, 256)
+LAST_CHUNKS = (1024, 1024, 1024, 640, 256, 128)
 VECTOR_CHUNKS = (3, 4)
 S_SPLIT = 320
 
@@ -104,7 +104,7 @@ def tile_picked_fpn_none_e_kernel(tc, xT, sT, w1, w2, offs, par, out):
         w2_mx = quantize_plain("w2", w2_raw, N, S_SPLIT // 2)
         coarse = []
         for m in range(M_TILES):
-            acc = ps.tile([P, V], F32, name="coarse_acc%d" % m)
+            acc = ps.tile([P, V], F32, name="coarse_acc%d" % m, tag="bank%d" % m)
             product(acc[:], w2_mx, m, (s_mx[0][:], s_mx[1][:]))
             t_rows = sb.tile([P, V], F32, name="coarse%d" % m)
             nc.scalar.copy(out=t_rows[:], in_=acc[:])
@@ -162,24 +162,30 @@ def tile_picked_fpn_none_e_kernel(tc, xT, sT, w1, w2, offs, par, out):
                 in_=picked[h][:, c0 * PACK : (c0 + PIECE) * PACK],
             )
 
-        def fine_product(w_mx, m, first, count):
-            acc = ps.tile([P, count], F32, name="fine_acc%d_%d" % (m, first))
-            product(acc[:], w_mx, 0, (x_codes[:, first : first + count], x_scales[:, first : first + count]))
-            return acc
+        accs = {}
 
-        def finish(acc, m, first, count):
-            h, c0 = divmod(first, HALF)
+        def fine_product(w_mx, m, first):
+            acc = ps.tile([P, PIECE], F32, name="fine_acc%d_%d" % (m, first), tag="bank%d" % ((len(accs) + M_TILES) % 8))
+            product(acc[:], w_mx, 0, (x_codes[:, first : first + PIECE], x_scales[:, first : first + PIECE]))
+            accs.setdefault((m, first), acc)
+
+        def finish(m, first, count):
             result = sb.tile([P, count], F32, name="result%d_%d" % (m, first))
-            nc.vector.tensor_tensor(result[:], acc[:], parents[h, m][:, c0 : c0 + count], ADD)
+            for c in range(0, count, PIECE):
+                h, c0 = divmod(first + c, HALF)
+                nc.vector.tensor_tensor(
+                    result[:, c : c + PIECE], accs[m, first + c][:], parents[h, m][:, c0 : c0 + PIECE], ADD
+                )
             nc.sync.dma_start(out=out[m * P : (m + 1) * P, first : first + count], in_=result[:])
 
-        units = []
         w1_mx = quantize("w1_0", w1_grouped[0][:], P)
         for first in range(0, S, PIECE):
             quantize_piece(first)
-            units.append((fine_product(w1_mx, 0, first, PIECE), 0, first, PIECE))
+            fine_product(w1_mx, 0, first)
         w1_mx = quantize("w1_1", w1_grouped[1][:], P)
+        for first in range(0, S, PIECE):
+            fine_product(w1_mx, 1, first)
+        for first in range(0, S, PIECE):
+            finish(0, first, PIECE)
         for first in range(0, S, HALF):
-            units.append((fine_product(w1_mx, 1, first, HALF), 1, first, HALF))
-        for unit in units:
-            finish(*unit)
+            finish(1, first, HALF)

@@ -98,7 +98,13 @@ def tile_picked_fpn_none_e_kernel(tc, xT, sT, w1, w2, offs, par, out):
             nc.sync.dma_start(out=row3[:, cols], in_=x_rows[:, 3, cols])
             last_cols.append(cols)
             c0 = c0 + width
-        w1_raw = [load_packed("w1_%d" % m, w1[:, m * P : (m + 1) * P], P) for m in range(M_TILES)]
+        w1_rows = w1.rearrange("(p t) c -> p t c", t=PACK)
+        w1_pairs = []
+        for u in range(2):
+            pair = sb.tile([P, 2, P], F32, name="w1_pair%d" % u, tag="w1_pair%d" % u, align_bytes=64)
+            nc.sync.dma_start(out=pair[:], in_=w1_rows[:, 2 * u : 2 * u + 2, 0:P])
+            w1_pairs.append(pair)
+        w1_second = load_packed("w1_1", w1[:, P : 2 * P], P)
 
         s_mx = quantize_plain("s", s_raw, V, S_SPLIT)
         w2_mx = quantize_plain("w2", w2_raw, N, S_SPLIT // 2)
@@ -148,9 +154,11 @@ def tile_picked_fpn_none_e_kernel(tc, xT, sT, w1, w2, offs, par, out):
         nc.scalar.activation(slot(1, 3), row3_bf[:].indirect(entries(offs_tile, HALF, HALF)), COPY)
 
         w1_grouped = [sb.tile([P, P * PACK], BF16, name="w1_grouped%d" % m, align_bytes=64) for m in range(M_TILES)]
-        gpsimd_copy(w1_grouped[0][:].rearrange("p (c t) -> p c t", t=PACK), w1_raw[0][:].rearrange("p t c -> p c t"))
-        interleave(nc.scalar.copy, w1_grouped[1], w1_raw[1], 0, P)
-        x_codes = sb.tile([P, S], U32, name="x_codes", tag="w1_0_raw", align_bytes=64)
+        for u, pair in enumerate(w1_pairs):
+            slots = w1_grouped[0][:].rearrange("p (c t) -> p c t", t=PACK)[:, :, 2 * u : 2 * u + 2]
+            gpsimd_copy(slots, pair[:].rearrange("p t c -> p c t"))
+        interleave(nc.scalar.copy, w1_grouped[1], w1_second, 0, P)
+        x_codes = sb.tile([P, S], U32, name="x_codes", tag="w1_pair1", align_bytes=64)
         x_scales = sb.tile([P, S], U8, name="x_scales", align_bytes=64)
 
         def quantize_piece(first):

@@ -20,8 +20,8 @@ LIST_ROWS = 16
 HALF = S // 2
 PIECE = 256
 M_TILES = N // P
-LAST_CHUNKS = (1024, 1024, 1024, 640, 256, 128)
-VECTOR_CHUNKS = (3, 4)
+LAST_CHUNKS = (2688, 1024, 256, 128)
+VECTOR_SHARES = (1664, 512, 256, 0)
 S_SPLIT = 320
 
 
@@ -84,10 +84,8 @@ def tile_picked_fpn_none_e_kernel(tc, xT, sT, w1, w2, offs, par, out):
         nc.sync.dma_start(par_tile[:], par)
         offs_tile = sb.tile([P, S // LIST_ROWS], U16, name="offs_tile")
         nc.sync.dma_start(offs_tile[:], offs)
-        row0 = sb.tile([P, T], F32, name="row0")
-        nc.sync.dma_start(out=row0[:], in_=x_rows[:, 0, :])
-        row1 = sb.tile([P, T], F32, name="row1", tag="row1")
-        nc.sync.dma_start(out=row1[:], in_=x_rows[:, 1, :])
+        rows01 = sb.tile([P, 2, T], F32, name="rows01")
+        nc.sync.dma_start(out=rows01[:], in_=x_rows[:, 0:2, :])
         row2 = sb.tile([P, T], F32, name="row2")
         nc.sync.dma_start(out=row2[:], in_=x_rows[:, 2, :])
         row3 = sb.tile([P, T], F32, name="row3")
@@ -123,32 +121,31 @@ def tile_picked_fpn_none_e_kernel(tc, xT, sT, w1, w2, offs, par, out):
                 nc.vector.tensor_copy(parents[:, c0 : c0 + PIECE], window)
             return parents
 
-        parents = {(h, m): fetch_parents(h, m, "parents%d_%d" % (h, m)) for h, m in ((0, 0), (1, 0), (0, 1))}
+        parents = {(h, m): fetch_parents(h, m, "parents%d_%d" % (h, m)) for m in range(M_TILES) for h in range(2)}
 
         picked = [sb.tile([P, HALF * PACK], BF16, name="picked%d" % h, align_bytes=64) for h in range(2)]
 
         def slot(h, t):
             return picked[h][:].rearrange("p (c t) -> p c t", t=PACK)[:, :, t]
 
-        low = sb.tile([P, 2, S], BF16, name="low")
-        nc.vector.tensor_copy(low[:, 0, :], row0[:].indirect(offs_tile[:]))
         for h in range(2):
-            cols = slice(h * HALF, (h + 1) * HALF)
-            nc.vector.tensor_copy(low[:, 1, cols], row1[:].indirect(entries(offs_tile, h * HALF, HALF)))
+            low = sb.tile([P, 2, HALF], F32, name="low%d" % h)
+            for t in range(2):
+                nc.vector.tensor_copy(low[:, t, :], rows01[:, t, :].indirect(entries(offs_tile, h * HALF, HALF)))
             nc.scalar.copy(
                 out=picked[h][:].rearrange("p (c t) -> p c t", t=PACK)[:, :, 0:2],
-                in_=low[:, :, cols].rearrange("p t c -> p c t"),
+                in_=low[:].rearrange("p t c -> p c t"),
             )
-        parents.setdefault((1, 1), fetch_parents(1, 1, "row1"))
         for h in (1, 0):
             nc.vector.tensor_copy(slot(h, 2), row2[:].indirect(entries(offs_tile, h * HALF, HALF)))
 
         row3_bf = sb.tile([P, T], BF16, name="row3_bf")
-        for index, cols in enumerate(last_cols):
-            if index in VECTOR_CHUNKS:
-                nc.vector.tensor_copy(out=row3_bf[:, cols], in_=row3[:, cols])
-            else:
-                nc.scalar.copy(out=row3_bf[:, cols], in_=row3[:, cols])
+        for cols, share in zip(last_cols, VECTOR_SHARES):
+            middle = cols.start + share
+            if share > 0:
+                nc.vector.tensor_copy(out=row3_bf[:, cols.start : middle], in_=row3[:, cols.start : middle])
+            if middle < cols.stop:
+                nc.scalar.copy(out=row3_bf[:, middle : cols.stop], in_=row3[:, middle : cols.stop])
 
         nc.vector.tensor_copy(slot(0, 3), row3[:].indirect(entries(offs_tile, 0, HALF)))
         nc.scalar.activation(slot(1, 3), row3_bf[:].indirect(entries(offs_tile, HALF, HALF)), COPY)

@@ -13,6 +13,7 @@ U8 = mybir.dt.uint8
 FP8X4 = mybir.dt.float8_e4m3fn_x4
 COPY = mybir.ActivationFunctionType.Copy
 ADD = mybir.AluOpType.add
+MULT = mybir.AluOpType.mult
 
 P = 128
 PACK = 4
@@ -20,8 +21,9 @@ LIST_ROWS = 16
 HALF = S // 2
 PIECE = 256
 M_TILES = N // P
-LAST_CHUNKS = (2688, 1024, 256, 128)
-VECTOR_SHARES = (1664, 512, 256, 0)
+LAST_LOADS = (2048, 1152, 512, 256, 128)
+VECTOR_SHARES = (768, 768, 384, 256, 0)
+SCALAR_SHARE = 2560
 S_SPLIT = 320
 
 
@@ -45,10 +47,10 @@ def tile_picked_fpn_none_e_kernel(tc, xT, sT, w1, w2, offs, par, out):
         ps = ctx.enter_context(tc.psum_pool(name="ps", bufs=1))
 
         def gpsimd_copy(out, in_):
-            nc.gpsimd.tensor_scalar(out=out, in0=in_, scalar1=1.0, scalar2=0.0, op0=mybir.AluOpType.mult, op1=ADD)
+            nc.gpsimd.tensor_scalar(out=out, in0=in_, scalar1=1.0, scalar2=0.0, op0=MULT, op1=ADD)
 
         def load_packed(name, src, width):
-            raw = sb.tile([P, PACK, width], F32, name=name + "_raw", tag=name + "_raw", align_bytes=64)
+            raw = sb.tile([P, PACK, width], F32, name=name + "_raw", align_bytes=64)
             nc.sync.dma_start(out=raw[:], in_=src.rearrange("(p t) c -> p t c", t=PACK))
             return raw
 
@@ -60,10 +62,8 @@ def tile_picked_fpn_none_e_kernel(tc, xT, sT, w1, w2, offs, par, out):
 
         def quantize_plain(name, raw, width, split):
             grouped = sb.tile([P, width * PACK], BF16, name=name + "_grouped", align_bytes=64)
-            if split > 0:
-                interleave(nc.vector.tensor_copy, grouped, raw, 0, split)
-            if split < width:
-                interleave(nc.scalar.copy, grouped, raw, split, width)
+            interleave(nc.vector.tensor_copy, grouped, raw, 0, split)
+            interleave(nc.scalar.copy, grouped, raw, split, width)
             return quantize(name, grouped[:], width)
 
         def product(acc, w, m, x):
@@ -84,16 +84,16 @@ def tile_picked_fpn_none_e_kernel(tc, xT, sT, w1, w2, offs, par, out):
         nc.sync.dma_start(par_tile[:], par)
         offs_tile = sb.tile([P, S // LIST_ROWS], U16, name="offs_tile")
         nc.sync.dma_start(offs_tile[:], offs)
-        rows01 = sb.tile([P, 2, T], F32, name="rows01")
-        nc.sync.dma_start(out=rows01[:], in_=x_rows[:, 0:2, :])
-        row2 = sb.tile([P, T], F32, name="row2")
-        nc.sync.dma_start(out=row2[:], in_=x_rows[:, 2, :])
-        row3 = sb.tile([P, T], F32, name="row3")
+        planes12 = sb.tile([P, 2, T], F32, name="planes12")
+        nc.sync.dma_start(out=planes12[:], in_=x_rows[:, 1:3, :])
+        plane0 = sb.tile([P, T], F32, name="plane0")
+        nc.sync.dma_start(out=plane0[:], in_=x_rows[:, 0, :])
+        plane3 = sb.tile([P, T], F32, name="plane3")
         c0 = 0
         last_cols = []
-        for width in LAST_CHUNKS:
+        for width in LAST_LOADS:
             cols = slice(c0, c0 + width)
-            nc.sync.dma_start(out=row3[:, cols], in_=x_rows[:, 3, cols])
+            nc.sync.dma_start(out=plane3[:, cols], in_=x_rows[:, 3, cols])
             last_cols.append(cols)
             c0 = c0 + width
         w1_rows = w1.rearrange("(p t) c -> p t c", t=PACK)
@@ -106,49 +106,46 @@ def tile_picked_fpn_none_e_kernel(tc, xT, sT, w1, w2, offs, par, out):
 
         s_mx = quantize_plain("s", s_raw, V, S_SPLIT)
         w2_mx = quantize_plain("w2", w2_raw, N, S_SPLIT // 2)
-        coarse = []
+        parents = {}
         for m in range(M_TILES):
             acc = ps.tile([P, V], F32, name="coarse_acc%d" % m, tag="bank%d" % m)
             product(acc[:], w2_mx, m, (s_mx[0][:], s_mx[1][:]))
-            t_rows = sb.tile([P, V], F32, name="coarse%d" % m)
-            nc.scalar.copy(out=t_rows[:], in_=acc[:])
-            coarse.append(t_rows)
-
-        def fetch_parents(h, m, tag):
-            parents = sb.tile([P, HALF], F32, name="parents%d_%d" % (h, m), tag=tag)
-            for c0 in range(0, HALF, PIECE):
-                window = coarse[m][:].indirect(entries(par_tile, h * HALF + c0, PIECE))
-                nc.vector.tensor_copy(parents[:, c0 : c0 + PIECE], window)
-            return parents
-
-        parents = {(h, m): fetch_parents(h, m, "parents%d_%d" % (h, m)) for m in range(M_TILES) for h in range(2)}
+            coarse = sb.tile([P, V], F32, name="coarse%d" % m)
+            nc.scalar.copy(out=coarse[:], in_=acc[:])
+            fetched = sb.tile([P, S], F32, name="parents%d" % m)
+            for first in range(0, S, PIECE):
+                window = coarse[:].indirect(entries(par_tile, first, PIECE))
+                nc.vector.tensor_copy(fetched[:, first : first + PIECE], window)
+            parents.setdefault(m, fetched)
 
         picked = [sb.tile([P, HALF * PACK], BF16, name="picked%d" % h, align_bytes=64) for h in range(2)]
 
         def slot(h, t):
             return picked[h][:].rearrange("p (c t) -> p c t", t=PACK)[:, :, t]
 
-        for h in range(2):
-            low = sb.tile([P, 2, HALF], F32, name="low%d" % h)
-            for t in range(2):
-                nc.vector.tensor_copy(low[:, t, :], rows01[:, t, :].indirect(entries(offs_tile, h * HALF, HALF)))
-            nc.scalar.copy(
-                out=picked[h][:].rearrange("p (c t) -> p c t", t=PACK)[:, :, 0:2],
-                in_=low[:].rearrange("p t c -> p c t"),
-            )
-        for h in (1, 0):
-            nc.vector.tensor_copy(slot(h, 2), row2[:].indirect(entries(offs_tile, h * HALF, HALF)))
+        def half_list(h):
+            return entries(offs_tile, h * HALF, HALF)
 
-        row3_bf = sb.tile([P, T], BF16, name="row3_bf")
+        plane2_bf = sb.tile([P, T], BF16, name="plane2_bf", tag="rounded")
+        nc.scalar.copy(out=plane2_bf[:, 0:SCALAR_SHARE], in_=planes12[:, 1, 0:SCALAR_SHARE])
+        gpsimd_copy(plane2_bf[:, SCALAR_SHARE:T], planes12[:, 1, SCALAR_SHARE:T])
+        for h in range(2):
+            nc.scalar.activation(slot(h, 2), plane2_bf[:].indirect(half_list(h)), COPY)
+        for h in range(2):
+            nc.vector.tensor_copy(slot(h, 1), planes12[:, 0, :].indirect(half_list(h)))
+        for h in range(2):
+            nc.vector.tensor_copy(slot(h, 0), plane0[:].indirect(half_list(h)))
+
+        plane3_bf = sb.tile([P, T], BF16, name="plane3_bf", tag="rounded")
         for cols, share in zip(last_cols, VECTOR_SHARES):
             middle = cols.start + share
             if share > 0:
-                nc.vector.tensor_copy(out=row3_bf[:, cols.start : middle], in_=row3[:, cols.start : middle])
+                nc.vector.tensor_copy(out=plane3_bf[:, cols.start : middle], in_=plane3[:, cols.start : middle])
             if middle < cols.stop:
-                nc.scalar.copy(out=row3_bf[:, middle : cols.stop], in_=row3[:, middle : cols.stop])
+                nc.scalar.copy(out=plane3_bf[:, middle : cols.stop], in_=plane3[:, middle : cols.stop])
 
-        nc.vector.tensor_copy(slot(0, 3), row3[:].indirect(entries(offs_tile, 0, HALF)))
-        nc.scalar.activation(slot(1, 3), row3_bf[:].indirect(entries(offs_tile, HALF, HALF)), COPY)
+        nc.vector.tensor_copy(slot(0, 3), plane3[:].indirect(half_list(0)))
+        nc.scalar.activation(slot(1, 3), plane3_bf[:].indirect(half_list(1)), COPY)
 
         w1_grouped = [sb.tile([P, P * PACK], BF16, name="w1_grouped%d" % m, align_bytes=64) for m in range(M_TILES)]
         for u, pair in enumerate(w1_pairs):
@@ -176,10 +173,9 @@ def tile_picked_fpn_none_e_kernel(tc, xT, sT, w1, w2, offs, par, out):
 
         def finish(m, first, count):
             result = sb.tile([P, count], F32, name="result%d_%d" % (m, first))
-            for c in range(0, count, PIECE):
-                h, c0 = divmod(first + c, HALF)
+            for c in range(first, first + count, PIECE):
                 nc.vector.tensor_tensor(
-                    result[:, c : c + PIECE], accs[m, first + c][:], parents[h, m][:, c0 : c0 + PIECE], ADD
+                    result[:, c - first : c - first + PIECE], accs[m, c][:], parents[m][:, c : c + PIECE], ADD
                 )
             nc.sync.dma_start(out=out[m * P : (m + 1) * P, first : first + count], in_=result[:])
 

@@ -22,7 +22,8 @@ HALF = S // 2
 PIECE = 256
 M_TILES = N // P
 LAST_LOADS = (2048, 1152, 512, 256, 128)
-VECTOR_SHARES = (768, 768, 384, 256, 0)
+VECTOR_SHARES = (0, 768, 384, 256, 0)
+GPSIMD_SHARES = (768, 0, 0, 0, 0)
 SCALAR_SHARE = 2560
 S_SPLIT = 320
 
@@ -137,12 +138,16 @@ def tile_picked_fpn_none_e_kernel(tc, xT, sT, w1, w2, offs, par, out):
             nc.vector.tensor_copy(slot(h, 0), plane0[:].indirect(half_list(h)))
 
         plane3_bf = sb.tile([P, T], BF16, name="plane3_bf", tag="rounded")
-        for cols, share in zip(last_cols, VECTOR_SHARES):
-            middle = cols.start + share
-            if share > 0:
-                nc.vector.tensor_copy(out=plane3_bf[:, cols.start : middle], in_=plane3[:, cols.start : middle])
-            if middle < cols.stop:
-                nc.scalar.copy(out=plane3_bf[:, middle : cols.stop], in_=plane3[:, middle : cols.stop])
+        for cols, vector_share, gpsimd_share in zip(last_cols, VECTOR_SHARES, GPSIMD_SHARES):
+            first_end = cols.start + vector_share
+            second_end = first_end + gpsimd_share
+            for copy, first, last in (
+                (nc.vector.tensor_copy, cols.start, first_end),
+                (gpsimd_copy, first_end, second_end),
+                (nc.scalar.copy, second_end, cols.stop),
+            ):
+                if first < last:
+                    copy(out=plane3_bf[:, first:last], in_=plane3[:, first:last])
 
         nc.vector.tensor_copy(slot(0, 3), plane3[:].indirect(half_list(0)))
         nc.scalar.activation(slot(1, 3), plane3_bf[:].indirect(half_list(1)), COPY)

@@ -20,11 +20,8 @@ PACK = 4
 LIST_ROWS = 16
 HALF = S // 2
 PIECE = 256
+PIECES = S // PIECE
 M_TILES = N // P
-LAST_LOADS = (2048, 1152, 512, 256, 128)
-VECTOR_SHARES = (0, 768, 384, 256, 0)
-GPSIMD_SHARES = (768, 0, 0, 0, 0)
-SCALAR_SHARE = 2560
 S_SPLIT = 320
 
 
@@ -45,13 +42,13 @@ def tile_picked_fpn_none_e_kernel(tc, xT, sT, w1, w2, offs, par, out):
 
     with ExitStack() as ctx:
         sb = ctx.enter_context(tc.tile_pool(name="sb", bufs=1))
+        shared = ctx.enter_context(tc.tile_pool(name="shared", bufs=1))
         ps = ctx.enter_context(tc.psum_pool(name="ps", bufs=1))
 
         def gpsimd_copy(out, in_):
             nc.gpsimd.tensor_scalar(out=out, in0=in_, scalar1=1.0, scalar2=0.0, op0=MULT, op1=ADD)
 
-        def load_packed(name, src, width):
-            raw = sb.tile([P, PACK, width], F32, name=name + "_raw", align_bytes=64)
+        def load_packed(raw, src):
             nc.sync.dma_start(out=raw[:], in_=src.rearrange("(p t) c -> p t c", t=PACK))
             return raw
 
@@ -79,31 +76,22 @@ def tile_picked_fpn_none_e_kernel(tc, xT, sT, w1, w2, offs, par, out):
                 stop=True,
             )
 
-        s_raw = load_packed("s", sT, V)
-        w2_raw = load_packed("w2", w2, N)
+        s_raw = load_packed(sb.tile([P, PACK, V], F32, name="s_raw"), sT)
+        w2_raw = load_packed(sb.tile([P, PACK, N], F32, name="w2_raw"), w2)
         par_tile = sb.tile([P, S // LIST_ROWS], U16, name="par_tile")
         nc.sync.dma_start(par_tile[:], par)
         offs_tile = sb.tile([P, S // LIST_ROWS], U16, name="offs_tile")
         nc.sync.dma_start(offs_tile[:], offs)
-        planes12 = sb.tile([P, 2, T], F32, name="planes12")
-        nc.sync.dma_start(out=planes12[:], in_=x_rows[:, 1:3, :])
-        plane0 = sb.tile([P, T], F32, name="plane0")
-        nc.sync.dma_start(out=plane0[:], in_=x_rows[:, 0, :])
+        planes01 = sb.tile([P, 2, T], F32, name="planes01")
+        nc.sync.dma_start(out=planes01[:], in_=x_rows[:, 0:2, :])
+        plane2 = sb.tile([P, T], F32, name="plane2")
+        nc.sync.dma_start(out=plane2[:], in_=x_rows[:, 2, :])
         plane3 = sb.tile([P, T], F32, name="plane3")
-        c0 = 0
-        last_cols = []
-        for width in LAST_LOADS:
-            cols = slice(c0, c0 + width)
-            nc.sync.dma_start(out=plane3[:, cols], in_=x_rows[:, 3, cols])
-            last_cols.append(cols)
-            c0 = c0 + width
-        w1_rows = w1.rearrange("(p t) c -> p t c", t=PACK)
-        w1_pairs = []
-        for u in range(2):
-            pair = sb.tile([P, 2, P], F32, name="w1_pair%d" % u, tag="w1_pair%d" % u, align_bytes=64)
-            nc.sync.dma_start(out=pair[:], in_=w1_rows[:, 2 * u : 2 * u + 2, 0:P])
-            w1_pairs.append(pair)
-        w1_second = load_packed("w1_1", w1[:, P : 2 * P], P)
+        nc.sync.dma_start(out=plane3[:], in_=x_rows[:, 3, :])
+        w1_raw = [
+            load_packed(shared.tile([P, PACK, P], F32, name="w1_raw0", offset=0, align_bytes=64), w1[:, 0:P]),
+            load_packed(sb.tile([P, PACK, P], F32, name="w1_raw1"), w1[:, P : 2 * P]),
+        ]
 
         s_mx = quantize_plain("s", s_raw, V, S_SPLIT)
         w2_mx = quantize_plain("w2", w2_raw, N, S_SPLIT // 2)
@@ -113,85 +101,101 @@ def tile_picked_fpn_none_e_kernel(tc, xT, sT, w1, w2, offs, par, out):
             product(acc[:], w2_mx, m, (s_mx[0][:], s_mx[1][:]))
             coarse = sb.tile([P, V], F32, name="coarse%d" % m)
             nc.scalar.copy(out=coarse[:], in_=acc[:])
-            fetched = sb.tile([P, S], F32, name="parents%d" % m)
-            for first in range(0, S, PIECE):
-                window = coarse[:].indirect(entries(par_tile, first, PIECE))
-                nc.vector.tensor_copy(fetched[:, first : first + PIECE], window)
-            parents.setdefault(m, fetched)
+            for c in range(PIECES):
+                tag = "parents%d_%d" % (m, c)
+                fetched = sb.tile([P, PIECE], F32, name=tag, tag=tag, align_bytes=64)
+                nc.vector.tensor_copy(fetched[:], coarse[:].indirect(entries(par_tile, c * PIECE, PIECE)))
+                parents.setdefault((m, c), fetched)
 
-        picked = [sb.tile([P, HALF * PACK], BF16, name="picked%d" % h, align_bytes=64) for h in range(2)]
+        first_half = sb.tile([P, HALF * PACK], BF16, name="first_half", align_bytes=64)
+        second_half = sb.tile([P, S + PIECE], F32, name="second_half", align_bytes=64)
+        picked = [first_half[:], second_half[:, 0:S].bitcast(BF16)]
 
-        def slot(h, t):
-            return picked[h][:].rearrange("p (c t) -> p c t", t=PACK)[:, :, t]
+        def slots(h):
+            return picked[h].rearrange("p (c t) -> p c t", t=PACK)
 
         def half_list(h):
             return entries(offs_tile, h * HALF, HALF)
 
-        plane2_bf = sb.tile([P, T], BF16, name="plane2_bf", tag="rounded")
-        nc.scalar.copy(out=plane2_bf[:, 0:SCALAR_SHARE], in_=planes12[:, 1, 0:SCALAR_SHARE])
-        gpsimd_copy(plane2_bf[:, SCALAR_SHARE:T], planes12[:, 1, SCALAR_SHARE:T])
-        for h in range(2):
-            nc.scalar.activation(slot(h, 2), plane2_bf[:].indirect(half_list(h)), COPY)
-        for h in range(2):
-            nc.vector.tensor_copy(slot(h, 1), planes12[:, 0, :].indirect(half_list(h)))
-        for h in range(2):
-            nc.vector.tensor_copy(slot(h, 0), plane0[:].indirect(half_list(h)))
+        for t, plane in enumerate((planes01[:, 0, :], planes01[:, 1, :], plane2[:], plane3[:])):
+            nc.vector.tensor_copy(slots(0)[:, :, t], plane.indirect(half_list(0)))
 
-        plane3_bf = sb.tile([P, T], BF16, name="plane3_bf", tag="rounded")
-        for cols, vector_share, gpsimd_share in zip(last_cols, VECTOR_SHARES, GPSIMD_SHARES):
-            first_end = cols.start + vector_share
-            second_end = first_end + gpsimd_share
-            for copy, first, last in (
-                (nc.vector.tensor_copy, cols.start, first_end),
-                (gpsimd_copy, first_end, second_end),
-                (nc.scalar.copy, second_end, cols.stop),
-            ):
-                if first < last:
-                    copy(out=plane3_bf[:, first:last], in_=plane3[:, first:last])
-
-        nc.vector.tensor_copy(slot(0, 3), plane3[:].indirect(half_list(0)))
-        nc.scalar.activation(slot(1, 3), plane3_bf[:].indirect(half_list(1)), COPY)
+        dense01 = sb.tile([P, 2, HALF], F32, name="dense01")
+        for t in range(2):
+            nc.scalar.activation(dense01[:, t, :], planes01[:, t, :].indirect(half_list(1)), COPY)
+        nc.scalar.copy(out=slots(1)[:, :, 0:2], in_=dense01[:].rearrange("p t c -> p c t"))
+        dense2 = sb.tile([P, HALF], BF16, name="dense2")
+        nc.scalar.activation(dense2[:], plane2[:].indirect(half_list(1)), COPY)
+        nc.scalar.copy(out=slots(1)[:, :, 2], in_=dense2[:])
 
         w1_grouped = [sb.tile([P, P * PACK], BF16, name="w1_grouped%d" % m, align_bytes=64) for m in range(M_TILES)]
-        for u, pair in enumerate(w1_pairs):
-            slots = w1_grouped[0][:].rearrange("p (c t) -> p c t", t=PACK)[:, :, 2 * u : 2 * u + 2]
-            gpsimd_copy(slots, pair[:].rearrange("p t c -> p c t"))
-        interleave(nc.scalar.copy, w1_grouped[1], w1_second, 0, P)
-        x_codes = sb.tile([P, S], U32, name="x_codes", tag="w1_pair1", align_bytes=64)
+        dense3a = sb.tile([P, PIECE], BF16, name="dense3a")
+        nc.scalar.activation(dense3a[:], plane3[:].indirect(entries(offs_tile, HALF, PIECE)), COPY)
+        gpsimd_copy(slots(1)[:, 0:PIECE, 3], dense3a[:])
+        interleave(nc.scalar.copy, w1_grouped[0], w1_raw[0], 0, P)
+        dense3b = shared.tile([P, PIECE], BF16, name="dense3b", offset=0, align_bytes=64)
+        nc.scalar.activation(dense3b[:], plane3[:].indirect(entries(offs_tile, HALF + PIECE, PIECE)), COPY)
+        interleave(nc.scalar.copy, w1_grouped[1], w1_raw[1], 0, P)
+        nc.scalar.copy(out=slots(1)[:, PIECE:HALF, 3], in_=dense3b[:])
+
+        early_codes = shared.tile([P, S - PIECE], U32, name="early_codes", offset=2 * PIECE, align_bytes=64)
+        x_codes = [early_codes[:, c * PIECE : (c + 1) * PIECE] for c in range(PIECES - 1)]
         x_scales = sb.tile([P, S], U8, name="x_scales", align_bytes=64)
 
-        def quantize_piece(first):
-            h, c0 = divmod(first, HALF)
-            cols = slice(first, first + PIECE)
+        def quantize_piece(c):
+            h, c0 = divmod(c * PIECE, HALF)
+            cols = slice(c * PIECE, (c + 1) * PIECE)
             nc.vector.quantize_mx(
-                out=x_codes[:, cols].bitcast(FP8X4),
+                out=x_codes[c].bitcast(FP8X4),
                 scales=x_scales[:, cols],
                 in_=picked[h][:, c0 * PACK : (c0 + PIECE) * PACK],
             )
 
         accs = {}
 
-        def fine_product(w_mx, m, first):
-            acc = ps.tile([P, PIECE], F32, name="fine_acc%d_%d" % (m, first), tag="bank%d" % ((len(accs) + M_TILES) % 8))
-            product(acc[:], w_mx, 0, (x_codes[:, first : first + PIECE], x_scales[:, first : first + PIECE]))
-            accs.setdefault((m, first), acc)
+        def fine_product(w_mx, m, c):
+            cols = slice(c * PIECE, (c + 1) * PIECE)
+            acc = ps.tile([P, PIECE], F32, name="fine_acc%d_%d" % (m, c), tag="bank%d" % ((len(accs) + M_TILES) % 8))
+            product(acc[:], w_mx, 0, (x_codes[c], x_scales[:, cols]))
+            accs.setdefault((m, c), acc)
 
-        def finish(m, first, count):
-            result = sb.tile([P, count], F32, name="result%d_%d" % (m, first))
-            for c in range(first, first + count, PIECE):
-                nc.vector.tensor_tensor(
-                    result[:, c - first : c - first + PIECE], accs[m, c][:], parents[m][:, c : c + PIECE], ADD
-                )
-            nc.sync.dma_start(out=out[m * P : (m + 1) * P, first : first + count], in_=result[:])
+        def add_on_vector(result, m, c):
+            cols = slice(c * PIECE, (c + 1) * PIECE)
+            nc.vector.tensor_tensor(result[:, cols], accs[m, c][:], parents[m, c][:], ADD)
 
-        w1_mx = quantize("w1_0", w1_grouped[0][:], P)
-        for first in range(0, S, PIECE):
-            quantize_piece(first)
-            fine_product(w1_mx, 0, first)
-        w1_mx = quantize("w1_1", w1_grouped[1][:], P)
-        for first in range(0, S, PIECE):
-            fine_product(w1_mx, 1, first)
-        for first in range(0, S, PIECE):
-            finish(0, first, PIECE)
-        for first in range(0, S, HALF):
-            finish(1, first, HALF)
+        def add_aside(result, m, c):
+            cols = slice(c * PIECE, (c + 1) * PIECE)
+            fine = sb.tile([P, PIECE], F32, name="fine%d_%d" % (m, c))
+            nc.scalar.copy(out=fine[:], in_=accs[m, c][:])
+            nc.gpsimd.tensor_tensor(result[:, cols], fine[:], parents[m, c][:], ADD)
+
+        def store(result, m, first, count):
+            cols = slice(first * PIECE, (first + count) * PIECE)
+            nc.sync.dma_start(out=out[m * P : (m + 1) * P, cols], in_=result[:, cols])
+
+        result0 = sb.tile([P, S], F32, name="result0")
+        result1 = second_half[:, PIECE : S + PIECE]
+        w1_mx0 = quantize("w1_0", w1_grouped[0][:], P)
+        for c in range(PIECES - 1):
+            quantize_piece(c)
+            fine_product(w1_mx0, 0, c)
+        w1_mx1 = quantize("w1_1", w1_grouped[1][:], P)
+        for c in range(PIECES - 1):
+            fine_product(w1_mx1, 1, c)
+        for c in range(PIECES - 1):
+            add_on_vector(result0, 0, c)
+            store(result0, 0, c, 1)
+        last_codes = sb.tile([P, PIECE], U32, name="last_codes", tag="parents0_1", align_bytes=64)
+        x_codes.append(last_codes[:])
+        quantize_piece(PIECES - 1)
+        fine_product(w1_mx0, 0, PIECES - 1)
+        fine_product(w1_mx1, 1, PIECES - 1)
+        add_on_vector(result1, 1, 0)
+        store(result1, 1, 0, 1)
+        add_aside(result1, 1, 1)
+        add_on_vector(result1, 1, 2)
+        store(result1, 1, 1, 2)
+        add_on_vector(result0, 0, 3)
+        store(result0, 0, 3, 1)
+        add_on_vector(result1, 1, 3)
+        store(result1, 1, 3, 1)

@@ -23,6 +23,8 @@ PIECE = 256
 PIECES = S // PIECE
 M_TILES = N // P
 S_SPLIT = 320
+EARLY = 256
+LAST = S - PIECE
 
 
 def entries(list_tile, first, count):
@@ -42,7 +44,6 @@ def tile_picked_fpn_none_e_kernel(tc, xT, sT, w1, w2, offs, par, out):
 
     with ExitStack() as ctx:
         sb = ctx.enter_context(tc.tile_pool(name="sb", bufs=1))
-        shared = ctx.enter_context(tc.tile_pool(name="shared", bufs=1))
         ps = ctx.enter_context(tc.psum_pool(name="ps", bufs=1))
 
         def gpsimd_copy(out, in_):
@@ -88,31 +89,36 @@ def tile_picked_fpn_none_e_kernel(tc, xT, sT, w1, w2, offs, par, out):
         nc.sync.dma_start(out=plane2[:], in_=x_rows[:, 2, :])
         plane3 = sb.tile([P, T], F32, name="plane3")
         nc.sync.dma_start(out=plane3[:], in_=x_rows[:, 3, :])
-        w1_raw = [
-            load_packed(shared.tile([P, PACK, P], F32, name="w1_raw0", offset=0, align_bytes=64), w1[:, 0:P]),
-            load_packed(sb.tile([P, PACK, P], F32, name="w1_raw1"), w1[:, P : 2 * P]),
-        ]
+        w1_rows = w1.rearrange("(p t) c -> p t c", t=PACK)
+        w1_pairs = []
+        for u in range(2):
+            pair = sb.tile([P, 2, P], F32, name="w1_pair%d" % u, tag="w1_pair%d" % u, align_bytes=64)
+            nc.sync.dma_start(out=pair[:], in_=w1_rows[:, 2 * u : 2 * u + 2, 0:P])
+            w1_pairs.append(pair)
+        w1_second = load_packed(sb.tile([P, PACK, P], F32, name="w1_second", tag="w1_second"), w1[:, P : 2 * P])
 
         s_mx = quantize_plain("s", s_raw, V, S_SPLIT)
         w2_mx = quantize_plain("w2", w2_raw, N, S_SPLIT // 2)
         parents = {}
+        last_parents = [sb.tile([P, M_TILES, P], F32, name="last_parents%d" % u) for u in range(2)]
         for m in range(M_TILES):
             acc = ps.tile([P, V], F32, name="coarse_acc%d" % m, tag="bank%d" % m)
             product(acc[:], w2_mx, m, (s_mx[0][:], s_mx[1][:]))
             coarse = sb.tile([P, V], F32, name="coarse%d" % m)
             nc.scalar.copy(out=coarse[:], in_=acc[:])
-            for c in range(PIECES):
+            for c in range(PIECES - 1):
                 tag = "parents%d_%d" % (m, c)
                 fetched = sb.tile([P, PIECE], F32, name=tag, tag=tag, align_bytes=64)
                 nc.vector.tensor_copy(fetched[:], coarse[:].indirect(entries(par_tile, c * PIECE, PIECE)))
                 parents.setdefault((m, c), fetched)
+            for u in range(2):
+                window = coarse[:].indirect(entries(par_tile, LAST + u * P, P))
+                nc.vector.tensor_copy(last_parents[u][:, m, :], window)
 
-        first_half = sb.tile([P, HALF * PACK], BF16, name="first_half", align_bytes=64)
-        second_half = sb.tile([P, S + PIECE], F32, name="second_half", align_bytes=64)
-        picked = [first_half[:], second_half[:, 0:S].bitcast(BF16)]
+        picked = [sb.tile([P, HALF * PACK], BF16, name="picked%d" % h, align_bytes=64) for h in range(2)]
 
         def slots(h):
-            return picked[h].rearrange("p (c t) -> p c t", t=PACK)
+            return picked[h][:].rearrange("p (c t) -> p c t", t=PACK)
 
         def half_list(h):
             return entries(offs_tile, h * HALF, HALF)
@@ -129,73 +135,78 @@ def tile_picked_fpn_none_e_kernel(tc, xT, sT, w1, w2, offs, par, out):
         nc.scalar.copy(out=slots(1)[:, :, 2], in_=dense2[:])
 
         w1_grouped = [sb.tile([P, P * PACK], BF16, name="w1_grouped%d" % m, align_bytes=64) for m in range(M_TILES)]
-        dense3a = sb.tile([P, PIECE], BF16, name="dense3a")
-        nc.scalar.activation(dense3a[:], plane3[:].indirect(entries(offs_tile, HALF, PIECE)), COPY)
-        gpsimd_copy(slots(1)[:, 0:PIECE, 3], dense3a[:])
-        interleave(nc.scalar.copy, w1_grouped[0], w1_raw[0], 0, P)
-        dense3b = shared.tile([P, PIECE], BF16, name="dense3b", offset=0, align_bytes=64)
-        nc.scalar.activation(dense3b[:], plane3[:].indirect(entries(offs_tile, HALF + PIECE, PIECE)), COPY)
-        interleave(nc.scalar.copy, w1_grouped[1], w1_raw[1], 0, P)
-        nc.scalar.copy(out=slots(1)[:, PIECE:HALF, 3], in_=dense3b[:])
+        def last_plane_on_scalar(dense, first, count):
+            runs = [(first, first + count // 2), (first + count // 2, first + count)]
+            for a, b in runs:
+                window = plane3[:].indirect(entries(offs_tile, HALF + a, b - a))
+                nc.scalar.activation(dense[:, a - first : b - first], window, COPY)
+            for a, b in runs:
+                nc.scalar.copy(out=slots(1)[:, a:b, 3], in_=dense[:, a - first : b - first])
 
-        early_codes = shared.tile([P, S - PIECE], U32, name="early_codes", offset=2 * PIECE, align_bytes=64)
-        x_codes = [early_codes[:, c * PIECE : (c + 1) * PIECE] for c in range(PIECES - 1)]
+        for u, pair in enumerate(w1_pairs):
+            pair_slots = w1_grouped[0][:].rearrange("p (c t) -> p c t", t=PACK)[:, :, 2 * u : 2 * u + 2]
+            gpsimd_copy(pair_slots, pair[:].rearrange("p t c -> p c t"))
+        last_plane_on_scalar(sb.tile([P, EARLY], F32, name="dense3_early"), 0, EARLY)
+        interleave(nc.scalar.copy, w1_grouped[1], w1_second, 0, P)
+        last_plane_on_scalar(sb.tile([P, HALF - EARLY], F32, name="dense3_late", tag="w1_second"), EARLY, HALF - EARLY)
+
+        early_codes = sb.tile([P, LAST], U32, name="early_codes", tag="w1_pair1", align_bytes=64)
         x_scales = sb.tile([P, S], U8, name="x_scales", align_bytes=64)
 
-        def quantize_piece(c):
-            h, c0 = divmod(c * PIECE, HALF)
-            cols = slice(c * PIECE, (c + 1) * PIECE)
+        def quantize_cells(codes, first, count):
+            h, c0 = divmod(first, HALF)
+            scales = x_scales[:, first : first + count]
             nc.vector.quantize_mx(
-                out=x_codes[c].bitcast(FP8X4),
-                scales=x_scales[:, cols],
-                in_=picked[h][:, c0 * PACK : (c0 + PIECE) * PACK],
+                out=codes.bitcast(FP8X4), scales=scales, in_=picked[h][:, c0 * PACK : (c0 + count) * PACK]
             )
+            return codes, scales
 
+        banks = [M_TILES]
+
+        def next_bank(name, shape):
+            banks.append(banks[-1] + 1)
+            return ps.tile(shape, F32, name=name, tag="bank%d" % (banks[-2] % 8))
+
+        def fine_product(m, c):
+            acc = next_bank("fine_acc%d_%d" % (m, c), [P, PIECE])
+            product(acc[:], w1_mx[m], 0, x_mx[c])
+            return acc
+
+        def finish(m, c):
+            result = sb.tile([P, PIECE], F32, name="result%d_%d" % (m, c))
+            nc.vector.tensor_tensor(result[:], accs[m, c][:], parents[m, c][:], ADD)
+            nc.sync.dma_start(out=out[m * P : (m + 1) * P, c * PIECE : (c + 1) * PIECE], in_=result[:])
+
+        def last_products(u, tag):
+            codes = sb.tile([P, P], U32, name="last_codes%d" % u, tag=tag, align_bytes=64)
+            cells_mx = quantize_cells(codes[:], LAST + u * P, P)
+            acc = next_bank("last_acc%d" % u, [P, M_TILES, P])
+            for m in range(M_TILES):
+                product(acc[:, m, :], w1_mx[m], 0, cells_mx)
+            return acc
+
+        def finish_last(u, acc):
+            result = sb.tile([P, M_TILES, P], F32, name="last_result%d" % u)
+            nc.vector.tensor_tensor(result[:], acc[:], last_parents[u][:], ADD)
+            cols = slice(LAST + u * P, LAST + (u + 1) * P)
+            nc.sync.dma_start(out=out.rearrange("(m p) c -> p m c", p=P)[:, :, cols], in_=result[:])
+
+        w1_mx = [quantize("w1_0", w1_grouped[0][:], P)]
+        x_mx = []
         accs = {}
-
-        def fine_product(w_mx, m, c):
-            cols = slice(c * PIECE, (c + 1) * PIECE)
-            acc = ps.tile([P, PIECE], F32, name="fine_acc%d_%d" % (m, c), tag="bank%d" % ((len(accs) + M_TILES) % 8))
-            product(acc[:], w_mx, 0, (x_codes[c], x_scales[:, cols]))
-            accs.setdefault((m, c), acc)
-
-        def add_on_vector(result, m, c):
-            cols = slice(c * PIECE, (c + 1) * PIECE)
-            nc.vector.tensor_tensor(result[:, cols], accs[m, c][:], parents[m, c][:], ADD)
-
-        def add_aside(result, m, c):
-            cols = slice(c * PIECE, (c + 1) * PIECE)
-            fine = sb.tile([P, PIECE], F32, name="fine%d_%d" % (m, c))
-            nc.scalar.copy(out=fine[:], in_=accs[m, c][:])
-            nc.gpsimd.tensor_tensor(result[:, cols], fine[:], parents[m, c][:], ADD)
-
-        def store(result, m, first, count):
-            cols = slice(first * PIECE, (first + count) * PIECE)
-            nc.sync.dma_start(out=out[m * P : (m + 1) * P, cols], in_=result[:, cols])
-
-        result0 = sb.tile([P, S], F32, name="result0")
-        result1 = second_half[:, PIECE : S + PIECE]
-        w1_mx0 = quantize("w1_0", w1_grouped[0][:], P)
         for c in range(PIECES - 1):
-            quantize_piece(c)
-            fine_product(w1_mx0, 0, c)
-        w1_mx1 = quantize("w1_1", w1_grouped[1][:], P)
+            x_mx.append(quantize_cells(early_codes[:, c * PIECE : (c + 1) * PIECE], c * PIECE, PIECE))
+            accs.setdefault((0, c), fine_product(0, c))
+        w1_mx.append(quantize("w1_1", w1_grouped[1][:], P))
         for c in range(PIECES - 1):
-            fine_product(w1_mx1, 1, c)
-        for c in range(PIECES - 1):
-            add_on_vector(result0, 0, c)
-            store(result0, 0, c, 1)
-        last_codes = sb.tile([P, PIECE], U32, name="last_codes", tag="parents0_1", align_bytes=64)
-        x_codes.append(last_codes[:])
-        quantize_piece(PIECES - 1)
-        fine_product(w1_mx0, 0, PIECES - 1)
-        fine_product(w1_mx1, 1, PIECES - 1)
-        add_on_vector(result1, 1, 0)
-        store(result1, 1, 0, 1)
-        add_aside(result1, 1, 1)
-        add_on_vector(result1, 1, 2)
-        store(result1, 1, 1, 2)
-        add_on_vector(result0, 0, 3)
-        store(result0, 0, 3, 1)
-        add_on_vector(result1, 1, 3)
-        store(result1, 1, 3, 1)
+            accs.setdefault((1, c), fine_product(1, c))
+        finish(0, 0)
+        finish(0, 1)
+        finish(0, 2)
+        finish(1, 0)
+        last_accs = [last_products(0, "parents0_2")]
+        finish(1, 1)
+        last_accs.append(last_products(1, "parents1_0"))
+        finish(1, 2)
+        for u in range(2):
+            finish_last(u, last_accs[u])

@@ -23,7 +23,6 @@ PIECE = 256
 PIECES = S // PIECE
 M_TILES = N // P
 S_SPLIT = 320
-EARLY = 256
 LAST = S - PIECE
 
 
@@ -100,20 +99,16 @@ def tile_picked_fpn_none_e_kernel(tc, xT, sT, w1, w2, offs, par, out):
         s_mx = quantize_plain("s", s_raw, V, S_SPLIT)
         w2_mx = quantize_plain("w2", w2_raw, N, S_SPLIT // 2)
         parents = {}
-        last_parents = [sb.tile([P, M_TILES, P], F32, name="last_parents%d" % u) for u in range(2)]
         for m in range(M_TILES):
             acc = ps.tile([P, V], F32, name="coarse_acc%d" % m, tag="bank%d" % m)
             product(acc[:], w2_mx, m, (s_mx[0][:], s_mx[1][:]))
             coarse = sb.tile([P, V], F32, name="coarse%d" % m)
             nc.scalar.copy(out=coarse[:], in_=acc[:])
-            for c in range(PIECES - 1):
+            for c in range(PIECES):
                 tag = "parents%d_%d" % (m, c)
                 fetched = sb.tile([P, PIECE], F32, name=tag, tag=tag, align_bytes=64)
                 nc.vector.tensor_copy(fetched[:], coarse[:].indirect(entries(par_tile, c * PIECE, PIECE)))
                 parents.setdefault((m, c), fetched)
-            for u in range(2):
-                window = coarse[:].indirect(entries(par_tile, LAST + u * P, P))
-                nc.vector.tensor_copy(last_parents[u][:, m, :], window)
 
         picked = [sb.tile([P, HALF * PACK], BF16, name="picked%d" % h, align_bytes=64) for h in range(2)]
 
@@ -135,20 +130,21 @@ def tile_picked_fpn_none_e_kernel(tc, xT, sT, w1, w2, offs, par, out):
         nc.scalar.copy(out=slots(1)[:, :, 2], in_=dense2[:])
 
         w1_grouped = [sb.tile([P, P * PACK], BF16, name="w1_grouped%d" % m, align_bytes=64) for m in range(M_TILES)]
-        def last_plane_on_scalar(dense, first, count):
-            runs = [(first, first + count // 2), (first + count // 2, first + count)]
-            for a, b in runs:
-                window = plane3[:].indirect(entries(offs_tile, HALF + a, b - a))
-                nc.scalar.activation(dense[:, a - first : b - first], window, COPY)
-            for a, b in runs:
-                nc.scalar.copy(out=slots(1)[:, a:b, 3], in_=dense[:, a - first : b - first])
+        def last_plane_on_scalar(runs, first):
+            for r, dense in enumerate(runs):
+                window = plane3[:].indirect(entries(offs_tile, HALF + first + r * P, P))
+                nc.scalar.activation(dense, window, COPY)
+            for r, dense in enumerate(runs):
+                nc.scalar.copy(out=slots(1)[:, first + r * P : first + (r + 1) * P, 3], in_=dense)
 
         for u, pair in enumerate(w1_pairs):
             pair_slots = w1_grouped[0][:].rearrange("p (c t) -> p c t", t=PACK)[:, :, 2 * u : 2 * u + 2]
             gpsimd_copy(pair_slots, pair[:].rearrange("p t c -> p c t"))
-        last_plane_on_scalar(sb.tile([P, EARLY], F32, name="dense3_early"), 0, EARLY)
-        interleave(nc.scalar.copy, w1_grouped[1], w1_second, 0, P)
-        last_plane_on_scalar(sb.tile([P, HALF - EARLY], F32, name="dense3_late", tag="w1_second"), EARLY, HALF - EARLY)
+        dense3 = sb.tile([P, 2, P], BF16, name="dense3")
+        last_plane_on_scalar([dense3[:, r, :] for r in range(2)], 0)
+        interleave(nc.scalar.copy, w1_grouped[1], w1_second, 0, P // 2)
+        interleave(nc.scalar.copy, w1_grouped[1], w1_second, P // 2, P)
+        last_plane_on_scalar([w1_second[:, r, 0 : P // 2].bitcast(BF16) for r in range(2)], PIECE)
 
         early_codes = sb.tile([P, LAST], U32, name="early_codes", tag="w1_pair1", align_bytes=64)
         x_scales = sb.tile([P, S], U8, name="x_scales", align_bytes=64)
@@ -172,24 +168,14 @@ def tile_picked_fpn_none_e_kernel(tc, xT, sT, w1, w2, offs, par, out):
             product(acc[:], w1_mx[m], 0, x_mx[c])
             return acc
 
-        def finish(m, c):
-            result = sb.tile([P, PIECE], F32, name="result%d_%d" % (m, c))
-            nc.vector.tensor_tensor(result[:], accs[m, c][:], parents[m, c][:], ADD)
-            nc.sync.dma_start(out=out[m * P : (m + 1) * P, c * PIECE : (c + 1) * PIECE], in_=result[:])
+        results = [sb.tile([P, S], F32, name="result%d" % m) for m in range(M_TILES)]
 
-        def last_products(u, tag):
-            codes = sb.tile([P, P], U32, name="last_codes%d" % u, tag=tag, align_bytes=64)
-            cells_mx = quantize_cells(codes[:], LAST + u * P, P)
-            acc = next_bank("last_acc%d" % u, [P, M_TILES, P])
-            for m in range(M_TILES):
-                product(acc[:, m, :], w1_mx[m], 0, cells_mx)
-            return acc
+        def add(m, c):
+            nc.vector.tensor_tensor(results[m][:, c * PIECE : (c + 1) * PIECE], accs[m, c][:], parents[m, c][:], ADD)
 
-        def finish_last(u, acc):
-            result = sb.tile([P, M_TILES, P], F32, name="last_result%d" % u)
-            nc.vector.tensor_tensor(result[:], acc[:], last_parents[u][:], ADD)
-            cols = slice(LAST + u * P, LAST + (u + 1) * P)
-            nc.sync.dma_start(out=out.rearrange("(m p) c -> p m c", p=P)[:, :, cols], in_=result[:])
+        def store(m, first, count):
+            cols = slice(first * PIECE, (first + count) * PIECE)
+            nc.sync.dma_start(out=out[m * P : (m + 1) * P, cols], in_=results[m][:, cols])
 
         w1_mx = [quantize("w1_0", w1_grouped[0][:], P)]
         x_mx = []
@@ -200,13 +186,27 @@ def tile_picked_fpn_none_e_kernel(tc, xT, sT, w1, w2, offs, par, out):
         w1_mx.append(quantize("w1_1", w1_grouped[1][:], P))
         for c in range(PIECES - 1):
             accs.setdefault((1, c), fine_product(1, c))
-        finish(0, 0)
-        finish(0, 1)
-        finish(0, 2)
-        finish(1, 0)
-        last_accs = [last_products(0, "parents0_2")]
-        finish(1, 1)
-        last_accs.append(last_products(1, "parents1_0"))
-        finish(1, 2)
-        for u in range(2):
-            finish_last(u, last_accs[u])
+        for m in range(M_TILES):
+            accs.setdefault((m, PIECES - 1), next_bank("fine_acc%d_last" % m, [P, PIECE]))
+
+        def last_products(u, tag):
+            codes = sb.tile([P, P], U32, name="last_codes%d" % u, tag=tag, align_bytes=64)
+            cells_mx = quantize_cells(codes[:], LAST + u * P, P)
+            for m in range(M_TILES):
+                product(accs[m, PIECES - 1][:, u * P : (u + 1) * P], w1_mx[m], 0, cells_mx)
+
+        for c in range(2):
+            add(0, c)
+            store(0, c, 1)
+        add(1, 0)
+        last_products(0, "parents0_1")
+        add(1, 1)
+        store(1, 0, 2)
+        last_products(1, "parents1_0")
+        add(1, 2)
+        store(1, 2, 1)
+        for c in range(2, 4):
+            add(0, c)
+        store(0, 2, 2)
+        add(1, 3)
+        store(1, 3, 1)

@@ -124,27 +124,35 @@ def tile_picked_fpn_none_e_kernel(tc, xT, sT, w1, w2, offs, par, out):
         dense01 = sb.tile([P, 2, HALF], F32, name="dense01")
         for t in range(2):
             nc.scalar.activation(dense01[:, t, :], planes01[:, t, :].indirect(half_list(1)), COPY)
-        nc.scalar.copy(out=slots(1)[:, :, 0:2], in_=dense01[:].rearrange("p t c -> p c t"))
+        gpsimd_copy(slots(1)[:, :, 0:2], dense01[:].rearrange("p t c -> p c t"))
         dense2 = sb.tile([P, HALF], BF16, name="dense2")
         nc.scalar.activation(dense2[:], plane2[:].indirect(half_list(1)), COPY)
         nc.scalar.copy(out=slots(1)[:, :, 2], in_=dense2[:])
 
         w1_grouped = [sb.tile([P, P * PACK], BF16, name="w1_grouped%d" % m, align_bytes=64) for m in range(M_TILES)]
-        def last_plane_on_scalar(runs, first):
-            for r, dense in enumerate(runs):
-                window = plane3[:].indirect(entries(offs_tile, HALF + first + r * P, P))
+        def gather_last_plane(runs):
+            for first, dense in runs:
+                window = plane3[:].indirect(entries(offs_tile, HALF + first, dense.shape[1]))
                 nc.scalar.activation(dense, window, COPY)
-            for r, dense in enumerate(runs):
-                nc.scalar.copy(out=slots(1)[:, first + r * P : first + (r + 1) * P, 3], in_=dense)
+
+        def lay_last_plane(copy, runs):
+            for first, dense in runs:
+                copy(out=slots(1)[:, first : first + dense.shape[1], 3], in_=dense)
 
         for u, pair in enumerate(w1_pairs):
             pair_slots = w1_grouped[0][:].rearrange("p (c t) -> p c t", t=PACK)[:, :, 2 * u : 2 * u + 2]
             gpsimd_copy(pair_slots, pair[:].rearrange("p t c -> p c t"))
         dense3 = sb.tile([P, 2, P], BF16, name="dense3")
-        last_plane_on_scalar([dense3[:, r, :] for r in range(2)], 0)
+        early_runs = [(r * P, dense3[:, r, :]) for r in range(2)]
+        gather_last_plane(early_runs)
+        lay_last_plane(nc.scalar.copy, early_runs)
         interleave(nc.scalar.copy, w1_grouped[1], w1_second, 0, P // 2)
         interleave(nc.scalar.copy, w1_grouped[1], w1_second, P // 2, P)
-        last_plane_on_scalar([w1_second[:, r, 0 : P // 2].bitcast(BF16) for r in range(2)], PIECE)
+        late_runs = [(PIECE, w1_second[:, 0, 0 : P // 2].bitcast(BF16))]
+        late_runs.extend((PIECE + P + r * P // 2, w1_second[:, 1 + r, 0 : P // 2]) for r in range(2))
+        gather_last_plane(late_runs)
+        lay_last_plane(gpsimd_copy, late_runs[:1])
+        lay_last_plane(nc.scalar.copy, late_runs[1:])
 
         early_codes = sb.tile([P, LAST], U32, name="early_codes", tag="w1_pair1", align_bytes=64)
         x_scales = sb.tile([P, S], U8, name="x_scales", align_bytes=64)
@@ -195,18 +203,18 @@ def tile_picked_fpn_none_e_kernel(tc, xT, sT, w1, w2, offs, par, out):
             for m in range(M_TILES):
                 product(accs[m, PIECES - 1][:, u * P : (u + 1) * P], w1_mx[m], 0, cells_mx)
 
-        for c in range(2):
-            add(0, c)
-            store(0, c, 1)
-        add(1, 0)
+        add(0, 0)
+        store(0, 0, 1)
+        add(0, 1)
+        add(0, 2)
+        store(0, 1, 2)
         last_products(0, "parents0_1")
+        add(1, 0)
+        store(1, 0, 1)
+        last_products(1, "parents0_2")
         add(1, 1)
-        store(1, 0, 2)
-        last_products(1, "parents1_0")
         add(1, 2)
-        store(1, 2, 1)
-        for c in range(2, 4):
-            add(0, c)
-        store(0, 2, 2)
-        add(1, 3)
-        store(1, 3, 1)
+        store(1, 1, 2)
+        for m in range(M_TILES):
+            add(m, 3)
+            store(m, 3, 1)

@@ -171,50 +171,45 @@ def tile_picked_fpn_none_e_kernel(tc, xT, sT, w1, w2, offs, par, out):
             banks.append(banks[-1] + 1)
             return ps.tile(shape, F32, name=name, tag="bank%d" % (banks[-2] % 8))
 
-        def fine_product(m, c):
-            acc = next_bank("fine_acc%d_%d" % (m, c), [P, PIECE])
-            product(acc[:], w1_mx[m], 0, x_mx[c])
-            return acc
-
         results = [sb.tile([P, S], F32, name="result%d" % m) for m in range(M_TILES)]
 
-        def add(m, c):
-            nc.vector.tensor_tensor(results[m][:, c * PIECE : (c + 1) * PIECE], accs[m, c][:], parents[m, c][:], ADD)
+        def add(m, first, count, acc):
+            c, c0 = divmod(first, PIECE)
+            nc.vector.tensor_tensor(results[m][:, first : first + count], acc, parents[m, c][:, c0 : c0 + count], ADD)
 
         def store(m, first, count):
-            cols = slice(first * PIECE, (first + count) * PIECE)
-            nc.sync.dma_start(out=out[m * P : (m + 1) * P, cols], in_=results[m][:, cols])
+            nc.sync.dma_start(out=out[m * P : (m + 1) * P, first : first + count], in_=results[m][:, first : first + count])
 
         w1_mx = [quantize("w1_0", w1_grouped[0][:], P)]
-        x_mx = []
-        accs = {}
-        for c in range(PIECES - 1):
-            x_mx.append(quantize_cells(early_codes[:, c * PIECE : (c + 1) * PIECE], c * PIECE, PIECE))
-            accs.setdefault((0, c), fine_product(0, c))
+        first_accs = [next_bank("first_acc%d" % u, [P, P]) for u in range(2)]
+        accs = {(0, c): next_bank("fine_acc0_%d" % c, [P, PIECE]) for c in range(1, PIECES - 1)}
+        for first in range(0, LAST, P):
+            cells_mx = quantize_cells(early_codes[:, first : first + P], first, P)
+            c, c0 = divmod(first, PIECE)
+            product(first_accs[c0 // P][:] if c == 0 else accs[0, c][:, c0 : c0 + P], w1_mx[0], 0, cells_mx)
         w1_mx.append(quantize("w1_1", w1_grouped[1][:], P))
         for c in range(PIECES - 1):
-            accs.setdefault((1, c), fine_product(1, c))
+            cols = slice(c * PIECE, (c + 1) * PIECE)
+            accs.setdefault((1, c), next_bank("fine_acc1_%d" % c, [P, PIECE]))
+            product(accs[1, c][:], w1_mx[1], 0, (early_codes[:, cols], x_scales[:, cols]))
+        for u in range(2):
+            add(0, u * P, P, first_accs[u][:])
+        store(0, 0, PIECE)
+        for c in range(1, PIECES - 1):
+            add(0, c * PIECE, PIECE, accs[0, c][:])
+        store(0, PIECE, 2 * PIECE)
         for m in range(M_TILES):
             accs.setdefault((m, PIECES - 1), next_bank("fine_acc%d_last" % m, [P, PIECE]))
-
-        def last_products(u, tag):
-            codes = sb.tile([P, P], U32, name="last_codes%d" % u, tag=tag, align_bytes=64)
-            cells_mx = quantize_cells(codes[:], LAST + u * P, P)
+        last_codes = sb.tile([P, PIECE], U32, name="last_codes", tag="parents0_1", align_bytes=64)
+        for c0 in range(0, PIECE, P):
+            cells_mx = quantize_cells(last_codes[:, c0 : c0 + P], LAST + c0, P)
             for m in range(M_TILES):
-                product(accs[m, PIECES - 1][:, u * P : (u + 1) * P], w1_mx[m], 0, cells_mx)
-
-        add(0, 0)
-        store(0, 0, 1)
-        add(0, 1)
-        add(0, 2)
-        store(0, 1, 2)
-        last_products(0, "parents0_1")
-        add(1, 0)
-        store(1, 0, 1)
-        last_products(1, "parents0_2")
-        add(1, 1)
-        add(1, 2)
-        store(1, 1, 2)
-        for m in range(M_TILES):
-            add(m, 3)
-            store(m, 3, 1)
+                product(accs[m, PIECES - 1][:, c0 : c0 + P], w1_mx[m], 0, cells_mx)
+        for c in range(PIECES - 1):
+            add(1, c * PIECE, PIECE, accs[1, c][:])
+            if c < 2:
+                store(1, c * PIECE, PIECE)
+        add(0, LAST, PIECE, accs[0, PIECES - 1][:])
+        store(0, LAST, PIECE)
+        add(1, LAST, PIECE, accs[1, PIECES - 1][:])
+        store(1, HALF, HALF)

@@ -88,12 +88,7 @@ def tile_picked_fpn_none_e_kernel(tc, xT, sT, w1, w2, offs, par, out):
         nc.sync.dma_start(out=plane2[:], in_=x_rows[:, 2, :])
         plane3 = sb.tile([P, T], F32, name="plane3")
         nc.sync.dma_start(out=plane3[:], in_=x_rows[:, 3, :])
-        w1_rows = w1.rearrange("(p t) c -> p t c", t=PACK)
-        w1_pairs = []
-        for u in range(2):
-            pair = sb.tile([P, 2, P], F32, name="w1_pair%d" % u, tag="w1_pair%d" % u, align_bytes=64)
-            nc.sync.dma_start(out=pair[:], in_=w1_rows[:, 2 * u : 2 * u + 2, 0:P])
-            w1_pairs.append(pair)
+        w1_first = load_packed(sb.tile([P, PACK, P], F32, name="w1_first", tag="w1_first", align_bytes=64), w1[:, 0:P])
         w1_second = load_packed(sb.tile([P, PACK, P], F32, name="w1_second", tag="w1_second"), w1[:, P : 2 * P])
 
         s_mx = quantize_plain("s", s_raw, V, S_SPLIT)
@@ -139,9 +134,7 @@ def tile_picked_fpn_none_e_kernel(tc, xT, sT, w1, w2, offs, par, out):
             for first, dense in runs:
                 copy(out=slots(1)[:, first : first + dense.shape[1], 3], in_=dense)
 
-        for u, pair in enumerate(w1_pairs):
-            pair_slots = w1_grouped[0][:].rearrange("p (c t) -> p c t", t=PACK)[:, :, 2 * u : 2 * u + 2]
-            gpsimd_copy(pair_slots, pair[:].rearrange("p t c -> p c t"))
+        gpsimd_copy(w1_grouped[0][:].rearrange("p (c t) -> p c t", t=PACK), w1_first[:].rearrange("p t c -> p c t"))
         dense3 = sb.tile([P, 2, P], BF16, name="dense3")
         early_runs = [(r * P, dense3[:, r, :]) for r in range(2)]
         gather_last_plane(early_runs)
@@ -154,7 +147,7 @@ def tile_picked_fpn_none_e_kernel(tc, xT, sT, w1, w2, offs, par, out):
         lay_last_plane(gpsimd_copy, late_runs[:1])
         lay_last_plane(nc.scalar.copy, late_runs[1:])
 
-        early_codes = sb.tile([P, LAST], U32, name="early_codes", tag="w1_pair1", align_bytes=64)
+        early_codes = sb.tile([P, LAST], U32, name="early_codes", tag="w1_first", align_bytes=64)
         x_scales = sb.tile([P, S], U8, name="x_scales", align_bytes=64)
 
         def quantize_cells(codes, first, count):
@@ -207,9 +200,8 @@ def tile_picked_fpn_none_e_kernel(tc, xT, sT, w1, w2, offs, par, out):
                 product(accs[m, PIECES - 1][:, c0 : c0 + P], w1_mx[m], 0, cells_mx)
         for c in range(PIECES - 1):
             add(1, c * PIECE, PIECE, accs[1, c][:])
-            if c < 2:
-                store(1, c * PIECE, PIECE)
+            store(1, c * PIECE, PIECE)
         add(0, LAST, PIECE, accs[0, PIECES - 1][:])
         store(0, LAST, PIECE)
         add(1, LAST, PIECE, accs[1, PIECES - 1][:])
-        store(1, HALF, HALF)
+        store(1, LAST, PIECE)

from contextlib import ExitStack

import concourse.mybir as mybir

K, T, S, V, N = 512, 4096, 1024, 512, 256
FLOPS = 2 * K * N * (S + V)

F32 = mybir.dt.float32
BF16 = mybir.dt.bfloat16
U32 = mybir.dt.uint32
U16 = mybir.dt.uint16
U8 = mybir.dt.uint8
FP8X4 = mybir.dt.float8_e4m3fn_x4
COPY = mybir.ActivationFunctionType.Copy
ADD = mybir.AluOpType.add
MULT = mybir.AluOpType.mult

P = 128
PACK = 4
LIST_ROWS = 16
HALF = S // 2
PIECE = 256
PIECES = S // PIECE
M_TILES = N // P
S_SPLIT = 320
LAST = S - PIECE


def entries(list_tile, first, count):
    return list_tile[:, first // LIST_ROWS : (first + count) // LIST_ROWS]


def interleave(copy, grouped, raw, first, last):
    copy(
        out=grouped[:, first * PACK : last * PACK].rearrange("p (c i t) -> p c t i", i=4, t=PACK),
        in_=raw[:, :, first:last].rearrange("p t (c i) -> p c t i", i=4),
    )


def tile_picked_fpn_none_e_kernel(tc, xT, sT, w1, w2, offs, par, out):
    nc = tc.nc
    x_rows = xT.rearrange("(p t) c -> p t c", t=PACK)

    with ExitStack() as ctx:
        sb = ctx.enter_context(tc.tile_pool(name="sb", bufs=1))
        ps = ctx.enter_context(tc.psum_pool(name="ps", bufs=1))

        def gpsimd_copy(out, in_):
            nc.gpsimd.tensor_scalar(out=out, in0=in_, scalar1=1.0, scalar2=0.0, op0=MULT, op1=ADD)

        def load_packed(raw, src):
            nc.sync.dma_start(out=raw[:], in_=src.rearrange("(p t) c -> p t c", t=PACK))
            return raw

        def quantize(name, grouped, width):
            codes = sb.tile([P, width], U32, name=name + "_codes", align_bytes=64)
            scales = sb.tile([P, width], U8, name=name + "_scales", align_bytes=64)
            nc.vector.quantize_mx(out=codes[:].bitcast(FP8X4), scales=scales[:], in_=grouped)
            return codes, scales

        def quantize_plain(name, raw, width, split):
            grouped = sb.tile([P, width * PACK], BF16, name=name + "_grouped", align_bytes=64)
            interleave(nc.vector.tensor_copy, grouped, raw, 0, split)
            interleave(nc.scalar.copy, grouped, raw, split, width)
            return quantize(name, grouped[:], width)

        def product(acc, w, m, x):
            cols = slice(m * P, (m + 1) * P)
            nc.tensor.matmul_mx(
                out=acc,
                lhsT=w[0][:, cols].bitcast(FP8X4),
                lhsT_scale=w[1][:, cols],
                rhs=x[0].bitcast(FP8X4),
                rhs_scale=x[1],
                start=True,
                stop=True,
            )

        s_raw = load_packed(sb.tile([P, PACK, V], F32, name="s_raw"), sT)
        w2_raw = load_packed(sb.tile([P, PACK, N], F32, name="w2_raw"), w2)
        par_tile = sb.tile([P, S // LIST_ROWS], U16, name="par_tile")
        nc.sync.dma_start(par_tile[:], par)
        offs_tile = sb.tile([P, S // LIST_ROWS], U16, name="offs_tile")
        nc.sync.dma_start(offs_tile[:], offs)
        planes01 = sb.tile([P, 2, T], F32, name="planes01")
        nc.sync.dma_start(out=planes01[:], in_=x_rows[:, 0:2, :])
        plane2 = sb.tile([P, T], F32, name="plane2")
        nc.sync.dma_start(out=plane2[:], in_=x_rows[:, 2, :])
        plane3 = sb.tile([P, T], F32, name="plane3")
        nc.sync.dma_start(out=plane3[:], in_=x_rows[:, 3, :])
        w1_first = load_packed(sb.tile([P, PACK, P], F32, name="w1_first", tag="w1_first", align_bytes=64), w1[:, 0:P])
        w1_second = load_packed(sb.tile([P, PACK, P], F32, name="w1_second", tag="w1_second"), w1[:, P : 2 * P])

        s_mx = quantize_plain("s", s_raw, V, S_SPLIT)
        w2_mx = quantize_plain("w2", w2_raw, N, S_SPLIT // 2)
        parents = {}
        for m in range(M_TILES):
            acc = ps.tile([P, V], F32, name="coarse_acc%d" % m, tag="bank%d" % m)
            product(acc[:], w2_mx, m, (s_mx[0][:], s_mx[1][:]))
            coarse = sb.tile([P, V], F32, name="coarse%d" % m)
            nc.scalar.copy(out=coarse[:], in_=acc[:])
            for c in range(PIECES):
                tag = "parents%d_%d" % (m, c)
                fetched = sb.tile([P, PIECE], F32, name=tag, tag=tag, align_bytes=64)
                nc.vector.tensor_copy(fetched[:], coarse[:].indirect(entries(par_tile, c * PIECE, PIECE)))
                parents.setdefault((m, c), fetched)

        picked = [sb.tile([P, HALF * PACK], BF16, name="picked%d" % h, align_bytes=64) for h in range(2)]

        def slots(h):
            return picked[h][:].rearrange("p (c t) -> p c t", t=PACK)

        def half_list(h):
            return entries(offs_tile, h * HALF, HALF)

        for t, plane in enumerate((planes01[:, 0, :], planes01[:, 1, :], plane2[:], plane3[:])):
            nc.vector.tensor_copy(slots(0)[:, :, t], plane.indirect(half_list(0)))

        dense01 = sb.tile([P, 2, HALF], F32, name="dense01")
        for t in range(2):
            nc.scalar.activation(dense01[:, t, :], planes01[:, t, :].indirect(half_list(1)), COPY)
        gpsimd_copy(slots(1)[:, :, 0:2], dense01[:].rearrange("p t c -> p c t"))
        dense2 = sb.tile([P, HALF], BF16, name="dense2")
        nc.scalar.activation(dense2[:], plane2[:].indirect(half_list(1)), COPY)
        nc.scalar.copy(out=slots(1)[:, :, 2], in_=dense2[:])

        w1_grouped = [sb.tile([P, P * PACK], BF16, name="w1_grouped%d" % m, align_bytes=64) for m in range(M_TILES)]
        def gather_last_plane(runs):
            for first, dense in runs:
                window = plane3[:].indirect(entries(offs_tile, HALF + first, dense.shape[1]))
                nc.scalar.activation(dense, window, COPY)

        def lay_last_plane(copy, runs):
            for first, dense in runs:
                copy(out=slots(1)[:, first : first + dense.shape[1], 3], in_=dense)

        gpsimd_copy(w1_grouped[0][:].rearrange("p (c t) -> p c t", t=PACK), w1_first[:].rearrange("p t c -> p c t"))
        dense3 = sb.tile([P, 2, P], BF16, name="dense3")
        early_runs = [(r * P, dense3[:, r, :]) for r in range(2)]
        gather_last_plane(early_runs)
        lay_last_plane(nc.scalar.copy, early_runs)
        interleave(nc.scalar.copy, w1_grouped[1], w1_second, 0, P // 2)
        interleave(nc.scalar.copy, w1_grouped[1], w1_second, P // 2, P)
        late_runs = [(PIECE, w1_second[:, 0, 0 : P // 2].bitcast(BF16))]
        late_runs.extend((PIECE + P + r * P // 2, w1_second[:, 1 + r, 0 : P // 2]) for r in range(2))
        gather_last_plane(late_runs)
        lay_last_plane(gpsimd_copy, late_runs[:1])
        lay_last_plane(nc.scalar.copy, late_runs[1:])

        early_codes = sb.tile([P, LAST], U32, name="early_codes", tag="w1_first", align_bytes=64)
        x_scales = sb.tile([P, S], U8, name="x_scales", align_bytes=64)

        def quantize_cells(codes, first, count):
            h, c0 = divmod(first, HALF)
            scales = x_scales[:, first : first + count]
            nc.vector.quantize_mx(
                out=codes.bitcast(FP8X4), scales=scales, in_=picked[h][:, c0 * PACK : (c0 + count) * PACK]
            )
            return codes, scales

        banks = [M_TILES]

        def next_bank(name, shape):
            banks.append(banks[-1] + 1)
            return ps.tile(shape, F32, name=name, tag="bank%d" % (banks[-2] % 8))

        results = [sb.tile([P, S], F32, name="result%d" % m) for m in range(M_TILES)]

        def add(m, first, count, acc):
            c, c0 = divmod(first, PIECE)
            nc.vector.tensor_tensor(results[m][:, first : first + count], acc, parents[m, c][:, c0 : c0 + count], ADD)

        def store(m, first, count):
            nc.sync.dma_start(out=out[m * P : (m + 1) * P, first : first + count], in_=results[m][:, first : first + count])

        w1_mx = [quantize("w1_0", w1_grouped[0][:], P)]
        first_accs = [next_bank("first_acc%d" % u, [P, P]) for u in range(2)]
        accs = {(0, c): next_bank("fine_acc0_%d" % c, [P, PIECE]) for c in range(1, PIECES - 1)}
        for first in range(0, LAST, P):
            cells_mx = quantize_cells(early_codes[:, first : first + P], first, P)
            c, c0 = divmod(first, PIECE)
            product(first_accs[c0 // P][:] if c == 0 else accs[0, c][:, c0 : c0 + P], w1_mx[0], 0, cells_mx)
        w1_mx.append(quantize("w1_1", w1_grouped[1][:], P))
        for c in range(PIECES - 1):
            cols = slice(c * PIECE, (c + 1) * PIECE)
            accs.setdefault((1, c), next_bank("fine_acc1_%d" % c, [P, PIECE]))
            product(accs[1, c][:], w1_mx[1], 0, (early_codes[:, cols], x_scales[:, cols]))
        for u in range(2):
            add(0, u * P, P, first_accs[u][:])
        store(0, 0, PIECE)
        for c in range(1, PIECES - 1):
            add(0, c * PIECE, PIECE, accs[0, c][:])
        store(0, PIECE, 2 * PIECE)
        for m in range(M_TILES):
            accs.setdefault((m, PIECES - 1), next_bank("fine_acc%d_last" % m, [P, PIECE]))
        last_codes = sb.tile([P, PIECE], U32, name="last_codes", tag="parents0_1", align_bytes=64)
        for c0 in range(0, PIECE, P):
            cells_mx = quantize_cells(last_codes[:, c0 : c0 + P], LAST + c0, P)
            for m in range(M_TILES):
                product(accs[m, PIECES - 1][:, c0 : c0 + P], w1_mx[m], 0, cells_mx)
        for c in range(PIECES - 1):
            add(1, c * PIECE, PIECE, accs[1, c][:])
            store(1, c * PIECE, PIECE)
        add(0, LAST, PIECE, accs[0, PIECES - 1][:])
        store(0, LAST, PIECE)
        add(1, LAST, PIECE, accs[1, PIECES - 1][:])
        store(1, LAST, PIECE)
